import numpy as np
import ml_dtypes


def mxq(x, axis, fmt="e4m3"):
    dtype, down = {"e4m3": (ml_dtypes.float8_e4m3fn, 7), "e5m2": (ml_dtypes.float8_e5m2, 14)}[fmt]
    v = np.moveaxis(np.asarray(x, np.float32).astype(ml_dtypes.bfloat16).astype(np.float64), axis, -1)
    blocks = v.reshape(v.shape[:-1] + (-1, 32))
    amax = np.abs(blocks).max(-1, keepdims=True)
    byte = np.maximum(np.where(amax > 0, np.frexp(amax)[1] - 1 + 127, 0) - down, 1)
    scale = np.exp2(byte - 127.0)
    codes = (blocks / scale).astype(np.float32).astype(dtype).astype(np.float64)
    return np.moveaxis((codes * scale).reshape(v.shape), -1, axis)


WIDE = False


def mx_kscale(k):
    if not WIDE:
        return np.ones(k)
    levels = np.array([10, -10, 5, -5, 0])
    if k % 512:
        return np.exp2(np.random.permutation(np.resize(levels, k // 32))).repeat(32)
    a = np.empty((k // 512, 16))
    for p in range(k // 512):
        a[p, :8] = np.random.permutation(np.resize(levels, 8))
        for g in range(8):
            far = levels[np.abs(levels - a[p, g]) >= 10]
            a[p, g + 8] = far[np.random.randint(len(far))]
    return np.exp2(a.ravel()).repeat(32)


def f64(x):
    return np.asarray(x).astype(np.float64)


def striped(idx):
    return np.tile(idx.reshape(-1, 16).T, (8, 1)).astype(np.uint16)


def unstriped(offs):
    return offs[:16].T.reshape(-1).astype(np.int64)


def relu(v):
    return np.maximum(v, 0.0)


K, T, D, S, V, N = 2048, 1024, 3, 512, 256, 256


def setup_inputs():
    n = np.random.standard_normal
    s = mx_kscale(K)[:, None]
    return {
        "xT": (n((K, T)) * s).astype(np.float32),
        "w": (n((K, N)) / np.sqrt(K) / s).astype(np.float32),
        "b": (0.3 * n((N, 1))).astype(np.float32),
        "gate": np.tile(np.random.uniform(0.2, 1.0, (D, 1, V)) / np.sqrt(D), (1, N, 1)).astype(np.float32),
        "offs": striped(np.random.permutation(T)[:S]),
        "pos1": striped(np.random.permutation(S)[:V]),
        "pos2": striped(np.random.permutation(S)[:V]),
        "pos3": striped(np.random.permutation(S)[:V]),
    }


def reference(xT, w, b, gate, offs, pos1, pos2, pos3):
    idx = unstriped(offs)
    xq = mxq(f64(xT)[:, idx], 0, "e4m3")
    y = mxq(f64(w), 0, "e4m3").T @ xq
    y = relu(y + f64(b))
    return sum(f64(gate[d]) * y[:, unstriped(p)] for d, p in enumerate((pos1, pos2, pos3)))

@@ -1,0 +1,210 @@
+from contextlib import ExitStack
+
+import concourse.mybir as mybir
+
+K, T, D, S, V, N = 2048, 1024, 3, 512, 256, 256
+FLOPS = 2 * K * N * S
+
+F32 = mybir.dt.float32
+BF16 = mybir.dt.bfloat16
+I32 = mybir.dt.int32
+U32 = mybir.dt.uint32
+U16 = mybir.dt.uint16
+U8 = mybir.dt.uint8
+FP8X4 = mybir.dt.float8_e4m3fn_x4
+RELU = mybir.ActivationFunctionType.Relu
+MULT = mybir.AluOpType.mult
+ADD = mybir.AluOpType.add
+
+P = 128
+PACK = 4
+K_PASS = P * PACK
+PASSES = K // K_PASS
+LAST = PASSES - 1
+M_TILES = N // P
+HALF = S // 2
+W_BF_BYTES = P * PACK * 2
+SLOT_NODES = 6 * P
+SLOT_BYTES = SLOT_NODES * PACK * 2
+
+X_CHUNKS = (
+    [(a, t0, 512, ns) for a in range(LAST) for t0, ns in ((0, 512), (512, 256))]
+    + [(LAST, t0, 256, ns) for t0, ns in ((0, 256), (256, 256), (512, 128), (768, 128))]
+)
+WHOLE_W_PASSES = 2
+
+
+def interleave(copy, grouped, raw):
+    copy(
+        out=grouped.rearrange("p (c i) j -> p c j i", i=4),
+        in_=raw.rearrange("p j (c i) -> p c j i", i=4),
+    )
+
+
+def tile_picked_sub_lin_relu_sub_e_kernel(tc, xT, w, b, gate, offs, pos1, pos2, pos3, out):
+    nc = tc.nc
+    with ExitStack() as ctx:
+        keep = ctx.enter_context(tc.tile_pool(name="keep", bufs=1))
+        slots = ctx.enter_context(tc.tile_pool(name="slots", bufs=1))
+        after_m0 = ctx.enter_context(tc.tile_pool(name="after_m0", bufs=1))
+        psum = ctx.enter_context(tc.psum_pool(name="psum", bufs=1))
+
+        def held(shape, dtype, name):
+            return keep.tile(shape, dtype, name=name, align_bytes=64)
+
+        def placed(pool, shape, dtype, name, offset):
+            return pool.tile(shape, dtype, name=name, align_bytes=64, offset=offset)
+
+        offsets = held([P, S // 16], U16, "offsets")
+        places = [held([P, V // 16], U16, "places%d" % d) for d in range(D)]
+        bias = [held([P, 1], F32, "bias%d" % m) for m in range(M_TILES)]
+        gates = [held([P, D, V], F32, "gates%d" % m) for m in range(M_TILES)]
+        x_raw = [held([P, PACK, n], F32, "x_raw%d" % c) for c, (a, t0, n, ns) in enumerate(X_CHUNKS)]
+        node_words = [held([P, T], U32, "node_words%d" % a) for a in range(PASSES)]
+        node_scales = held([P, T], U8, "node_scales")
+        picked_scales = held([P, S], U8, "picked_scales")
+        last_slot = (len(X_CHUNKS) - 1) * SLOT_BYTES
+
+        warm_in = held([P, 8], F32, "warm_in")
+        warm_out = held([P, 8], F32, "warm_out")
+        nc.vector.memset(warm_in[:], 0.0)
+        nc.scalar.activation(out=warm_out[:], in_=warm_in[:], func=RELU)
+        nc.vector.memset(node_scales[:].bitcast(I32), 0)
+        for m in range(M_TILES):
+            nc.scalar.dma_start(out=bias[m][:], in_=b[m * P : (m + 1) * P, :])
+
+        def k_rows(src, a):
+            return src[a * K_PASS : (a + 1) * K_PASS, :].rearrange("(p j) c -> p j c", j=PACK)
+
+        for c, (a, t0, n, ns) in enumerate(X_CHUNKS):
+            nc.sync.dma_start(out=x_raw[c][:], in_=k_rows(xT, a)[:, :, t0 : t0 + n])
+            if c == 0:
+                nc.sync.dma_start(offsets[:], offs)
+
+        w_raw = {}
+        for a in range(WHOLE_W_PASSES):
+            whole = held([P, PACK, N], F32, "w_raw%d" % a)
+            nc.sync.dma_start(out=whole[:], in_=k_rows(w, a))
+            for m in range(M_TILES):
+                w_raw[(a, m)] = whole[:, :, m * P : (m + 1) * P]
+        for m in range(M_TILES):
+            for a in range(WHOLE_W_PASSES, PASSES):
+                part = held([P, PACK, P], F32, "w_raw%d_%d" % (a, m))
+                nc.sync.dma_start(out=part[:], in_=k_rows(w, a)[:, :, m * P : (m + 1) * P])
+                w_raw[(a, m)] = part[:]
+            if m == 0:
+                for d, pos in enumerate((pos1, pos2, pos3)):
+                    nc.sync.dma_start(places[d][:], pos)
+            nc.sync.dma_start(out=gates[m][:], in_=gate[:, m * P : (m + 1) * P, :].rearrange("d p v -> p d v"))
+
+        picked_words = {}
+
+        def gather_words(picked, a, j0, j1):
+            nc.vector.tensor_copy(picked[:], node_words[a][:].indirect(offsets[:, j0 // 16 : j1 // 16]))
+            for h in range(j0 // HALF, j1 // HALF):
+                picked_words[(a, h)] = picked[:, h * HALF - j0 : (h + 1) * HALF - j0]
+
+        def quantize_nodes(a, t0, n, grouped):
+            nc.vector.quantize_mx(
+                out=node_words[a][:, t0 : t0 + n].bitcast(FP8X4),
+                scales=node_scales[PACK * a : P, t0 : t0 + n],
+                in_=grouped[:, 0:n, :].rearrange("p t j -> p (t j)"),
+            )
+
+        for c, (a, t0, n, ns) in enumerate(X_CHUNKS):
+            by_scalar = placed(slots, [P, SLOT_NODES, PACK], BF16, "x_bf_scalar%d" % c, c * SLOT_BYTES)
+            interleave(nc.scalar.copy, by_scalar[:, 0:ns, :], x_raw[c][:, :, 0:ns])
+            if ns < n:
+                by_vector = placed(slots, [P, n - ns, PACK], BF16, "x_bf_vector%d" % c, (c - 1) * SLOT_BYTES)
+                interleave(nc.vector.tensor_copy, by_vector[:], x_raw[c][:, :, ns:n])
+                quantize_nodes(a, t0 + ns, n - ns, by_vector)
+            quantize_nodes(a, t0, ns, by_scalar)
+            if t0 + n == T and a < LAST:
+                gather_words(held([P, S], U32, "picked_words%d" % a), a, 0, S)
+
+        def w_slot(a, m):
+            return last_slot + (a + m * PASSES) * W_BF_BYTES
+
+        def weights_pass(a, m):
+            name = "%d_%d" % (a, m)
+            if m == 1 and a >= WHOLE_W_PASSES:
+                w_bf = placed(after_m0, [P, P, PACK], BF16, "w_bf" + name, (a - WHOLE_W_PASSES) * W_BF_BYTES)
+            else:
+                w_bf = placed(slots, [P, P, PACK], BF16, "w_bf" + name, w_slot(a, m))
+            if (a, m) == (LAST, 0):
+                w_words = placed(after_m0, [P, P], U32, "w_words" + name, W_BF_BYTES - 256)
+            else:
+                w_words = held([P, P], U32, "w_words" + name)
+            w_scales = held([P, P], U8, "w_scales" + name)
+            interleave(nc.scalar.copy, w_bf[:], w_raw[(a, m)])
+            nc.vector.quantize_mx(
+                out=w_words[:].bitcast(FP8X4),
+                scales=w_scales[:],
+                in_=w_bf[:].rearrange("p c j -> p (c j)"),
+            )
+            return w_words, w_scales
+
+        def multiply(acc, a, w_words, w_scales):
+            for h in range(2):
+                nc.tensor.matmul_mx(
+                    out=acc[h][:],
+                    lhsT=w_words[:].bitcast(FP8X4),
+                    lhsT_scale=w_scales[:],
+                    rhs=picked_words[(a, h)].bitcast(FP8X4),
+                    rhs_scale=picked_scales[PACK * a : P, h * HALF : (h + 1) * HALF],
+                    start=(a == 0),
+                    stop=(a == LAST),
+                )
+
+        def results(m, acc):
+            y = held([P, S], F32, "y%d" % m)
+            for h in range(2):
+                nc.scalar.activation(out=y[:, h * HALF : (h + 1) * HALF], in_=acc[h][:], func=RELU, bias=bias[m][:])
+            return y
+
+        def term(m, d, y):
+            name = "term%d_%d" % (m, d)
+            if m == 0 and d > 0:
+                product = placed(after_m0, [P, V], F32, name, (d - 1) * W_BF_BYTES)
+            else:
+                product = held([P, V], F32, name)
+            nc.vector.tensor_tensor(product[:], y[:].indirect(places[d][:]), gates[m][:, d, :], MULT)
+            return product
+
+        def add(first, second, name):
+            total = held([P, V], F32, name)
+            nc.vector.tensor_tensor(total[:], first[:], second[:], ADD)
+            return total
+
+        def store(m, total):
+            nc.sync.dma_start(out=out[m * P : (m + 1) * P, :], in_=total[:])
+
+        def accumulators():
+            return [psum.tile([P, HALF], F32, name="acc%d" % h) for h in range(2)]
+
+        nc.vector.tensor_copy(picked_scales[:], node_scales[:].indirect(offsets[:]))
+        acc0 = accumulators()
+        multiply(acc0, 0, *weights_pass(0, 0))
+        gather_words(placed(slots, [P, HALF], U32, "picked_last0", w_slot(0, 0)), LAST, 0, HALF)
+        early = [weights_pass(0, 1)]
+        multiply(acc0, 1, *weights_pass(1, 0))
+        gather_words(placed(slots, [P, HALF], U32, "picked_last1", w_slot(1, 0)), LAST, HALF, S)
+        multiply(acc0, 2, *weights_pass(2, 0))
+        multiply(acc0, 3, *weights_pass(3, 0))
+        early.append(weights_pass(1, 1))
+        y0 = results(0, acc0)
+        first0 = term(0, 0, y0)
+        acc1 = accumulators()
+        for a in range(WHOLE_W_PASSES):
+            multiply(acc1, a, *early[a])
+        multiply(acc1, 2, *weights_pass(2, 1))
+        multiply(acc1, 3, *weights_pass(3, 1))
+        y1 = results(1, acc1)
+        second0 = term(0, 1, y0)
+        third0 = term(0, 2, y0)
+        partial0 = add(first0, second0, "partial0")
+        first1 = term(1, 0, y1)
+        store(0, add(partial0, third0, "total0"))
+        second1 = term(1, 1, y1)
+        third1 = term(1, 2, y1)
+        store(1, add(add(first1, second1, "partial1"), third1, "total1"))

@@ -24,14 +24,14 @@ LAST = PASSES - 1
 M_TILES = N // P
 HALF = S // 2
 W_BF_BYTES = P * PACK * 2
-SLOT_NODES = 6 * P
+SLOT_NODES = PASSES * N
 SLOT_BYTES = SLOT_NODES * PACK * 2
 
 X_CHUNKS = (
-    [(a, t0, 512, ns) for a in range(LAST) for t0, ns in ((0, 512), (512, 256))]
-    + [(LAST, t0, 256, ns) for t0, ns in ((0, 256), (256, 256), (512, 128), (768, 128))]
+    [(a, 0, 512, (256, 256)) for a in range(LAST)]
+    + [(LAST, 0, 128, (256, 128)), (LAST, 512, 256, (128, 128))]
 )
-WHOLE_W_PASSES = 2
+W_PIECES = [(0, 0, N), (1, 0, N), (2, 0, P), (2, P, P), (3, 0, P), (3, P, P)]
 
 
 def interleave(copy, grouped, raw):
@@ -46,63 +46,45 @@ def tile_picked_sub_lin_relu_sub_e_kernel(tc, xT, w, b, gate, offs, pos1, pos2, 
     with ExitStack() as ctx:
         keep = ctx.enter_context(tc.tile_pool(name="keep", bufs=1))
         slots = ctx.enter_context(tc.tile_pool(name="slots", bufs=1))
-        after_m0 = ctx.enter_context(tc.tile_pool(name="after_m0", bufs=1))
         psum = ctx.enter_context(tc.psum_pool(name="psum", bufs=1))
 
         def held(shape, dtype, name):
             return keep.tile(shape, dtype, name=name, align_bytes=64)
 
-        def placed(pool, shape, dtype, name, offset):
-            return pool.tile(shape, dtype, name=name, align_bytes=64, offset=offset)
+        def placed(shape, dtype, name, offset):
+            return slots.tile(shape, dtype, name=name, align_bytes=64, offset=offset)
 
         offsets = held([P, S // 16], U16, "offsets")
         places = [held([P, V // 16], U16, "places%d" % d) for d in range(D)]
         bias = [held([P, 1], F32, "bias%d" % m) for m in range(M_TILES)]
         gates = [held([P, D, V], F32, "gates%d" % m) for m in range(M_TILES)]
-        x_raw = [held([P, PACK, n], F32, "x_raw%d" % c) for c, (a, t0, n, ns) in enumerate(X_CHUNKS)]
+        x_raw = [held([P, PACK, nv + sum(runs)], F32, "x_raw%d" % c) for c, (a, t0, nv, runs) in enumerate(X_CHUNKS)]
+        w_raw = [held([P, PACK, N], F32, "w_raw%d" % a) for a in range(PASSES)]
         node_words = [held([P, T], U32, "node_words%d" % a) for a in range(PASSES)]
         node_scales = held([P, T], U8, "node_scales")
         picked_scales = held([P, S], U8, "picked_scales")
-        last_slot = (len(X_CHUNKS) - 1) * SLOT_BYTES
 
         warm_in = held([P, 8], F32, "warm_in")
         warm_out = held([P, 8], F32, "warm_out")
         nc.vector.memset(warm_in[:], 0.0)
         nc.scalar.activation(out=warm_out[:], in_=warm_in[:], func=RELU)
         nc.vector.memset(node_scales[:].bitcast(I32), 0)
-        for m in range(M_TILES):
-            nc.scalar.dma_start(out=bias[m][:], in_=b[m * P : (m + 1) * P, :])
 
         def k_rows(src, a):
             return src[a * K_PASS : (a + 1) * K_PASS, :].rearrange("(p j) c -> p j c", j=PACK)
 
-        for c, (a, t0, n, ns) in enumerate(X_CHUNKS):
-            nc.sync.dma_start(out=x_raw[c][:], in_=k_rows(xT, a)[:, :, t0 : t0 + n])
+        for c, (a, t0, nv, runs) in enumerate(X_CHUNKS):
+            nc.sync.dma_start(out=x_raw[c][:], in_=k_rows(xT, a)[:, :, t0 : t0 + nv + sum(runs)])
             if c == 0:
                 nc.sync.dma_start(offsets[:], offs)
-
-        w_raw = {}
-        for a in range(WHOLE_W_PASSES):
-            whole = held([P, PACK, N], F32, "w_raw%d" % a)
-            nc.sync.dma_start(out=whole[:], in_=k_rows(w, a))
-            for m in range(M_TILES):
-                w_raw[(a, m)] = whole[:, :, m * P : (m + 1) * P]
+        for a in range(PASSES):
+            nc.sync.dma_start(out=w_raw[a][:], in_=k_rows(w, a))
         for m in range(M_TILES):
-            for a in range(WHOLE_W_PASSES, PASSES):
-                part = held([P, PACK, P], F32, "w_raw%d_%d" % (a, m))
-                nc.sync.dma_start(out=part[:], in_=k_rows(w, a)[:, :, m * P : (m + 1) * P])
-                w_raw[(a, m)] = part[:]
+            nc.sync.dma_start(out=bias[m][:], in_=b[m * P : (m + 1) * P, :])
             if m == 0:
                 for d, pos in enumerate((pos1, pos2, pos3)):
                     nc.sync.dma_start(places[d][:], pos)
             nc.sync.dma_start(out=gates[m][:], in_=gate[:, m * P : (m + 1) * P, :].rearrange("d p v -> p d v"))
-
-        picked_words = {}
-
-        def gather_words(picked, a, j0, j1):
-            nc.vector.tensor_copy(picked[:], node_words[a][:].indirect(offsets[:, j0 // 16 : j1 // 16]))
-            for h in range(j0 // HALF, j1 // HALF):
-                picked_words[(a, h)] = picked[:, h * HALF - j0 : (h + 1) * HALF - j0]
 
         def quantize_nodes(a, t0, n, grouped):
             nc.vector.quantize_mx(
@@ -111,63 +93,84 @@ def tile_picked_sub_lin_relu_sub_e_kernel(tc, xT, w, b, gate, offs, pos1, pos2, 
                 in_=grouped[:, 0:n, :].rearrange("p t j -> p (t j)"),
             )
 
-        for c, (a, t0, n, ns) in enumerate(X_CHUNKS):
-            by_scalar = placed(slots, [P, SLOT_NODES, PACK], BF16, "x_bf_scalar%d" % c, c * SLOT_BYTES)
-            interleave(nc.scalar.copy, by_scalar[:, 0:ns, :], x_raw[c][:, :, 0:ns])
-            if ns < n:
-                by_vector = placed(slots, [P, n - ns, PACK], BF16, "x_bf_vector%d" % c, (c - 1) * SLOT_BYTES)
-                interleave(nc.vector.tensor_copy, by_vector[:], x_raw[c][:, :, ns:n])
-                quantize_nodes(a, t0 + ns, n - ns, by_vector)
-            quantize_nodes(a, t0, ns, by_scalar)
-            if t0 + n == T and a < LAST:
+        picked_words = {}
+
+        def gather_words(picked, a, j0, j1):
+            nc.vector.tensor_copy(picked[:], node_words[a][:].indirect(offsets[:, j0 // 16 : j1 // 16]))
+            for h in range(j0 // HALF, j1 // HALF):
+                picked_words[(a, h)] = picked[:, h * HALF - j0 : (h + 1) * HALF - j0]
+
+        slot = 0
+        for c, (a, t0, nv, runs) in enumerate(X_CHUNKS):
+            by_vector = placed([P, nv, PACK], BF16, "x_bf_vector%d" % c, slot * SLOT_BYTES)
+            interleave(nc.vector.tensor_copy, by_vector[:], x_raw[c][:, :, 0:nv])
+            by_scalar = []
+            first = nv
+            for n in runs:
+                slot += 1
+                grouped = placed([P, SLOT_NODES, PACK], BF16, "x_bf_scalar%d" % slot, slot * SLOT_BYTES)
+                interleave(nc.scalar.copy, grouped[:, 0:n, :], x_raw[c][:, :, first : first + n])
+                by_scalar.append((first, n, grouped))
+                first += n
+            quantize_nodes(a, t0, nv, by_vector)
+            for first, n, grouped in by_scalar:
+                quantize_nodes(a, t0 + first, n, grouped)
+            if t0 + nv + sum(runs) == T and a < LAST:
                 gather_words(held([P, S], U32, "picked_words%d" % a), a, 0, S)
+        nc.vector.tensor_copy(picked_scales[:], node_scales[:].indirect(offsets[:]))
 
-        def w_slot(a, m):
-            return last_slot + (a + m * PASSES) * W_BF_BYTES
+        w_words = {}
+        w_scales = {}
 
-        def weights_pass(a, m):
-            name = "%d_%d" % (a, m)
-            if m == 1 and a >= WHOLE_W_PASSES:
-                w_bf = placed(after_m0, [P, P, PACK], BF16, "w_bf" + name, (a - WHOLE_W_PASSES) * W_BF_BYTES)
-            else:
-                w_bf = placed(slots, [P, P, PACK], BF16, "w_bf" + name, w_slot(a, m))
-            if (a, m) == (LAST, 0):
-                w_words = placed(after_m0, [P, P], U32, "w_words" + name, W_BF_BYTES - 256)
-            else:
-                w_words = held([P, P], U32, "w_words" + name)
-            w_scales = held([P, P], U8, "w_scales" + name)
-            interleave(nc.scalar.copy, w_bf[:], w_raw[(a, m)])
+        def w_offset(a, m0):
+            return (slot - len(X_CHUNKS[-1][3])) * SLOT_BYTES + (a * N + m0) * PACK * 2
+
+        w_bf = {}
+        for a, m0, rows in W_PIECES:
+            w_bf[(a, m0)] = placed([P, rows, PACK], BF16, "w_bf%d_%d" % (a, m0), w_offset(a, m0))
+            interleave(nc.scalar.copy, w_bf[(a, m0)][:], w_raw[a][:, :, m0 : m0 + rows])
+
+        def quantize_weights(a, m0, rows, words):
+            scales = held([P, rows], U8, "w_scales%d_%d" % (a, m0))
             nc.vector.quantize_mx(
-                out=w_words[:].bitcast(FP8X4),
-                scales=w_scales[:],
-                in_=w_bf[:].rearrange("p c j -> p (c j)"),
+                out=words[:].bitcast(FP8X4),
+                scales=scales[:],
+                in_=w_bf[(a, m0)][:].rearrange("p c j -> p (c j)"),
             )
-            return w_words, w_scales
+            for m in range(m0 // P, (m0 + rows) // P):
+                w_words[(a, m)] = words[:, m * P - m0 : (m + 1) * P - m0]
+                w_scales[(a, m)] = scales[:, m * P - m0 : (m + 1) * P - m0]
 
-        def multiply(acc, a, w_words, w_scales):
-            for h in range(2):
-                nc.tensor.matmul_mx(
-                    out=acc[h][:],
-                    lhsT=w_words[:].bitcast(FP8X4),
-                    lhsT_scale=w_scales[:],
-                    rhs=picked_words[(a, h)].bitcast(FP8X4),
-                    rhs_scale=picked_scales[PACK * a : P, h * HALF : (h + 1) * HALF],
-                    start=(a == 0),
-                    stop=(a == LAST),
-                )
+        quantize_weights(0, 0, N, held([P, N], U32, "w_words0"))
+        quantize_weights(1, 0, N, held([P, N], U32, "w_words1"))
+        gather_words(placed([P, HALF], U32, "picked_last0", w_offset(1, 0)), LAST, 0, HALF)
+        quantize_weights(2, 0, P, held([P, P], U32, "w_words2_0"))
+        gather_words(placed([P, HALF], U32, "picked_last1", w_offset(2, 0)), LAST, HALF, S)
+        quantize_weights(3, 0, P, held([P, P], U32, "w_words3_0"))
+        quantize_weights(2, P, P, placed([P, P], U32, "w_words2_1", w_offset(3, 0)))
+        quantize_weights(3, P, P, held([P, P], U32, "w_words3_1"))
 
-        def results(m, acc):
+        def results(m):
+            acc = [psum.tile([P, HALF], F32, name="acc%d" % h) for h in range(2)]
+            for a in range(PASSES):
+                for h in range(2):
+                    cols = slice(h * HALF, (h + 1) * HALF)
+                    nc.tensor.matmul_mx(
+                        out=acc[h][:],
+                        lhsT=w_words[(a, m)].bitcast(FP8X4),
+                        lhsT_scale=w_scales[(a, m)],
+                        rhs=picked_words[(a, h)].bitcast(FP8X4),
+                        rhs_scale=picked_scales[PACK * a : P, cols],
+                        start=(a == 0),
+                        stop=(a == LAST),
+                    )
             y = held([P, S], F32, "y%d" % m)
             for h in range(2):
                 nc.scalar.activation(out=y[:, h * HALF : (h + 1) * HALF], in_=acc[h][:], func=RELU, bias=bias[m][:])
             return y
 
         def term(m, d, y):
-            name = "term%d_%d" % (m, d)
-            if m == 0 and d > 0:
-                product = placed(after_m0, [P, V], F32, name, (d - 1) * W_BF_BYTES)
-            else:
-                product = held([P, V], F32, name)
+            product = held([P, V], F32, "term%d_%d" % (m, d))
             nc.vector.tensor_tensor(product[:], y[:].indirect(places[d][:]), gates[m][:, d, :], MULT)
             return product
 
@@ -179,32 +182,12 @@ def tile_picked_sub_lin_relu_sub_e_kernel(tc, xT, w, b, gate, offs, pos1, pos2, 
         def store(m, total):
             nc.sync.dma_start(out=out[m * P : (m + 1) * P, :], in_=total[:])
 
-        def accumulators():
-            return [psum.tile([P, HALF], F32, name="acc%d" % h) for h in range(2)]
-
-        nc.vector.tensor_copy(picked_scales[:], node_scales[:].indirect(offsets[:]))
-        acc0 = accumulators()
-        multiply(acc0, 0, *weights_pass(0, 0))
-        gather_words(placed(slots, [P, HALF], U32, "picked_last0", w_slot(0, 0)), LAST, 0, HALF)
-        early = [weights_pass(0, 1)]
-        multiply(acc0, 1, *weights_pass(1, 0))
-        gather_words(placed(slots, [P, HALF], U32, "picked_last1", w_slot(1, 0)), LAST, HALF, S)
-        multiply(acc0, 2, *weights_pass(2, 0))
-        multiply(acc0, 3, *weights_pass(3, 0))
-        early.append(weights_pass(1, 1))
-        y0 = results(0, acc0)
-        first0 = term(0, 0, y0)
-        acc1 = accumulators()
-        for a in range(WHOLE_W_PASSES):
-            multiply(acc1, a, *early[a])
-        multiply(acc1, 2, *weights_pass(2, 1))
-        multiply(acc1, 3, *weights_pass(3, 1))
-        y1 = results(1, acc1)
-        second0 = term(0, 1, y0)
-        third0 = term(0, 2, y0)
-        partial0 = add(first0, second0, "partial0")
+        y0 = results(0)
+        y1 = results(1)
+        terms0 = [term(0, d, y0) for d in range(D)]
+        partial0 = add(terms0[0], terms0[1], "partial0")
         first1 = term(1, 0, y1)
-        store(0, add(partial0, third0, "total0"))
+        store(0, add(partial0, terms0[2], "total0"))
         second1 = term(1, 1, y1)
         third1 = term(1, 2, y1)
         store(1, add(add(first1, second1, "partial1"), third1, "total1"))

@@ -23,21 +23,21 @@ PASSES = K // K_PASS
 LAST = PASSES - 1
 M_TILES = N // P
 HALF = S // 2
-W_BF_BYTES = P * PACK * 2
+W_RAW_BYTES = PACK * N * 4
 SLOT_NODES = PASSES * N
 SLOT_BYTES = SLOT_NODES * PACK * 2
 
 X_CHUNKS = (
-    [(a, 0, 512, (256, 256)) for a in range(LAST)]
+    [(0, 0, 512, (512,)), (1, 0, 512, (256, 256))]
+    + [(2, 0, 0, (512,)), (2, 512, 128, (256, 128))]
     + [(LAST, 0, 128, (256, 128)), (LAST, 512, 256, (128, 128))]
 )
-W_PIECES = [(0, 0, N), (1, 0, N), (2, 0, P), (2, P, P), (3, 0, P), (3, P, P)]
 
 
 def interleave(copy, grouped, raw):
     copy(
-        out=grouped.rearrange("p (c i) j -> p c j i", i=4),
-        in_=raw.rearrange("p j (c i) -> p c j i", i=4),
+        out=grouped.rearrange("p (c i) j -> p c j i", i=2),
+        in_=raw.rearrange("p j (c i) -> p c j i", i=2),
     )
 
 
@@ -46,6 +46,8 @@ def tile_picked_sub_lin_relu_sub_e_kernel(tc, xT, w, b, gate, offs, pos1, pos2, 
     with ExitStack() as ctx:
         keep = ctx.enter_context(tc.tile_pool(name="keep", bufs=1))
         slots = ctx.enter_context(tc.tile_pool(name="slots", bufs=1))
+        raw_w = ctx.enter_context(tc.tile_pool(name="raw_w", bufs=1))
+        after_relu = ctx.enter_context(tc.tile_pool(name="after_relu", bufs=1))
         psum = ctx.enter_context(tc.psum_pool(name="psum", bufs=1))
 
         def held(shape, dtype, name):
@@ -56,10 +58,10 @@ def tile_picked_sub_lin_relu_sub_e_kernel(tc, xT, w, b, gate, offs, pos1, pos2, 
 
         offsets = held([P, S // 16], U16, "offsets")
         places = [held([P, V // 16], U16, "places%d" % d) for d in range(D)]
-        bias = [held([P, 1], F32, "bias%d" % m) for m in range(M_TILES)]
+        bias = [held([P, 1], F32, "bias0"), after_relu.tile([P, 1], F32, name="bias1", offset=0)]
         gates = [held([P, D, V], F32, "gates%d" % m) for m in range(M_TILES)]
         x_raw = [held([P, PACK, nv + sum(runs)], F32, "x_raw%d" % c) for c, (a, t0, nv, runs) in enumerate(X_CHUNKS)]
-        w_raw = [held([P, PACK, N], F32, "w_raw%d" % a) for a in range(PASSES)]
+        w_raw = [raw_w.tile([P, PACK, N], F32, name="w_raw%d" % a, offset=a * W_RAW_BYTES) for a in range(PASSES)]
         node_words = [held([P, T], U32, "node_words%d" % a) for a in range(PASSES)]
         node_scales = held([P, T], U8, "node_scales")
         picked_scales = held([P, S], U8, "picked_scales")
@@ -69,6 +71,8 @@ def tile_picked_sub_lin_relu_sub_e_kernel(tc, xT, w, b, gate, offs, pos1, pos2, 
         nc.vector.memset(warm_in[:], 0.0)
         nc.scalar.activation(out=warm_out[:], in_=warm_in[:], func=RELU)
         nc.vector.memset(node_scales[:].bitcast(I32), 0)
+        for m in range(M_TILES):
+            nc.scalar.dma_start(out=bias[m][:], in_=b[m * P : (m + 1) * P, :])
 
         def k_rows(src, a):
             return src[a * K_PASS : (a + 1) * K_PASS, :].rearrange("(p j) c -> p j c", j=PACK)
@@ -80,7 +84,6 @@ def tile_picked_sub_lin_relu_sub_e_kernel(tc, xT, w, b, gate, offs, pos1, pos2, 
         for a in range(PASSES):
             nc.sync.dma_start(out=w_raw[a][:], in_=k_rows(w, a))
         for m in range(M_TILES):
-            nc.sync.dma_start(out=bias[m][:], in_=b[m * P : (m + 1) * P, :])
             if m == 0:
                 for d, pos in enumerate((pos1, pos2, pos3)):
                     nc.sync.dma_start(places[d][:], pos)
@@ -102,8 +105,11 @@ def tile_picked_sub_lin_relu_sub_e_kernel(tc, xT, w, b, gate, offs, pos1, pos2, 
 
         slot = 0
         for c, (a, t0, nv, runs) in enumerate(X_CHUNKS):
-            by_vector = placed([P, nv, PACK], BF16, "x_bf_vector%d" % c, slot * SLOT_BYTES)
-            interleave(nc.vector.tensor_copy, by_vector[:], x_raw[c][:, :, 0:nv])
+            own = []
+            if nv:
+                by_vector = placed([P, nv, PACK], BF16, "x_bf_vector%d" % c, slot * SLOT_BYTES)
+                interleave(nc.vector.tensor_copy, by_vector[:], x_raw[c][:, :, 0:nv])
+                own.append((0, nv, by_vector))
             by_scalar = []
             first = nv
             for n in runs:
@@ -112,43 +118,54 @@ def tile_picked_sub_lin_relu_sub_e_kernel(tc, xT, w, b, gate, offs, pos1, pos2, 
                 interleave(nc.scalar.copy, grouped[:, 0:n, :], x_raw[c][:, :, first : first + n])
                 by_scalar.append((first, n, grouped))
                 first += n
-            quantize_nodes(a, t0, nv, by_vector)
-            for first, n, grouped in by_scalar:
+            runs_ready = by_scalar[:1] + own + by_scalar[1:]
+            for first, n, grouped in runs_ready:
                 quantize_nodes(a, t0 + first, n, grouped)
             if t0 + nv + sum(runs) == T and a < LAST:
                 gather_words(held([P, S], U32, "picked_words%d" % a), a, 0, S)
         nc.vector.tensor_copy(picked_scales[:], node_scales[:].indirect(offsets[:]))
 
+        w_bf = {}
         w_words = {}
         w_scales = {}
 
-        def w_offset(a, m0):
-            return (slot - len(X_CHUNKS[-1][3])) * SLOT_BYTES + (a * N + m0) * PACK * 2
+        def w_slot(n):
+            return (slot - len(X_CHUNKS[-1][3])) * SLOT_BYTES + n * P * PACK * 2
 
-        w_bf = {}
-        for a, m0, rows in W_PIECES:
-            w_bf[(a, m0)] = placed([P, rows, PACK], BF16, "w_bf%d_%d" % (a, m0), w_offset(a, m0))
-            interleave(nc.scalar.copy, w_bf[(a, m0)][:], w_raw[a][:, :, m0 : m0 + rows])
+        def round_weights(copy, a, m0, tiles, offset, room=0):
+            grouped = placed([P, (tiles + room) * P, PACK], BF16, "w_bf%d_%d" % (a, m0), offset)
+            interleave(copy, grouped[:, 0 : tiles * P, :], w_raw[a][:, :, m0 * P : (m0 + tiles) * P])
+            for m in range(tiles):
+                w_bf[(a, m0 + m)] = grouped[:, m * P : (m + 1) * P, :]
 
-        def quantize_weights(a, m0, rows, words):
-            scales = held([P, rows], U8, "w_scales%d_%d" % (a, m0))
+        def quantize_weights(a, m):
+            name = "%d_%d" % (a, m)
+            words = held([P, P], U32, "w_words" + name)
+            if m == 1 and a < 2:
+                scales = placed([P, P], U8, "w_scales" + name, w_slot(7) + a * P)
+            else:
+                scales = held([P, P], U8, "w_scales" + name)
             nc.vector.quantize_mx(
                 out=words[:].bitcast(FP8X4),
                 scales=scales[:],
-                in_=w_bf[(a, m0)][:].rearrange("p c j -> p (c j)"),
+                in_=w_bf[(a, m)].rearrange("p c j -> p (c j)"),
             )
-            for m in range(m0 // P, (m0 + rows) // P):
-                w_words[(a, m)] = words[:, m * P - m0 : (m + 1) * P - m0]
-                w_scales[(a, m)] = scales[:, m * P - m0 : (m + 1) * P - m0]
+            w_words[(a, m)] = words[:]
+            w_scales[(a, m)] = scales[:]
 
-        quantize_weights(0, 0, N, held([P, N], U32, "w_words0"))
-        quantize_weights(1, 0, N, held([P, N], U32, "w_words1"))
-        gather_words(placed([P, HALF], U32, "picked_last0", w_offset(1, 0)), LAST, 0, HALF)
-        quantize_weights(2, 0, P, held([P, P], U32, "w_words2_0"))
-        gather_words(placed([P, HALF], U32, "picked_last1", w_offset(2, 0)), LAST, HALF, S)
-        quantize_weights(3, 0, P, held([P, P], U32, "w_words3_0"))
-        quantize_weights(2, P, P, placed([P, P], U32, "w_words2_1", w_offset(3, 0)))
-        quantize_weights(3, P, P, held([P, P], U32, "w_words3_1"))
+        round_weights(nc.scalar.copy, 0, 0, 2, w_slot(2))
+        round_weights(nc.scalar.copy, 1, 0, 2, w_slot(0))
+        round_weights(nc.scalar.copy, 2, 0, 1, w_slot(4))
+        round_weights(nc.scalar.copy, 3, 0, 1, w_slot(5), room=2)
+        for a in range(PASSES):
+            quantize_weights(a, 0)
+            if a < 2:
+                picked = raw_w.tile([P, HALF], U32, name="picked_last%d" % a, align_bytes=64, offset=a * W_RAW_BYTES)
+                gather_words(picked, LAST, a * HALF, (a + 1) * HALF)
+        round_weights(nc.scalar.copy, 2, 1, 1, w_slot(5))
+        round_weights(nc.vector.tensor_copy, 3, 1, 1, w_slot(6))
+        for a in (0, 1, 3, 2):
+            quantize_weights(a, 1)
 
         def results(m):
             acc = [psum.tile([P, HALF], F32, name="acc%d" % h) for h in range(2)]
@@ -174,8 +191,7 @@ def tile_picked_sub_lin_relu_sub_e_kernel(tc, xT, w, b, gate, offs, pos1, pos2, 
             nc.vector.tensor_tensor(product[:], y[:].indirect(places[d][:]), gates[m][:, d, :], MULT)
             return product
 
-        def add(first, second, name):
-            total = held([P, V], F32, name)
+        def add(first, second, total):
             nc.vector.tensor_tensor(total[:], first[:], second[:], ADD)
             return total
 
@@ -185,9 +201,9 @@ def tile_picked_sub_lin_relu_sub_e_kernel(tc, xT, w, b, gate, offs, pos1, pos2, 
         y0 = results(0)
         y1 = results(1)
         terms0 = [term(0, d, y0) for d in range(D)]
-        partial0 = add(terms0[0], terms0[1], "partial0")
+        partial0 = add(terms0[0], terms0[1], held([P, V], F32, "partial0"))
         first1 = term(1, 0, y1)
-        store(0, add(partial0, terms0[2], "total0"))
+        store(0, add(partial0, terms0[2], after_relu.tile([P, V], F32, name="total0", offset=0)))
         second1 = term(1, 1, y1)
         third1 = term(1, 2, y1)
-        store(1, add(add(first1, second1, "partial1"), third1, "total1"))
+        store(1, add(add(first1, second1, held([P, V], F32, "partial1")), third1, held([P, V], F32, "total1")))

@@ -61,7 +61,8 @@ def tile_picked_sub_lin_relu_sub_e_kernel(tc, xT, w, b, gate, offs, pos1, pos2, 
         bias = [held([P, 1], F32, "bias0"), after_relu.tile([P, 1], F32, name="bias1", offset=0)]
         gates = [held([P, D, V], F32, "gates%d" % m) for m in range(M_TILES)]
         x_raw = [held([P, PACK, nv + sum(runs)], F32, "x_raw%d" % c) for c, (a, t0, nv, runs) in enumerate(X_CHUNKS)]
-        w_raw = [raw_w.tile([P, PACK, N], F32, name="w_raw%d" % a, offset=a * W_RAW_BYTES) for a in range(PASSES)]
+        w_raw = [raw_w.tile([P, PACK, N], F32, name="w_raw%d" % a, offset=a * W_RAW_BYTES) for a in range(LAST)]
+        w_last = [held([P, PACK, P], F32, "w_last%d" % m) for m in range(M_TILES)]
         node_words = [held([P, T], U32, "node_words%d" % a) for a in range(PASSES)]
         node_scales = held([P, T], U8, "node_scales")
         picked_scales = held([P, S], U8, "picked_scales")
@@ -81,8 +82,10 @@ def tile_picked_sub_lin_relu_sub_e_kernel(tc, xT, w, b, gate, offs, pos1, pos2, 
             nc.sync.dma_start(out=x_raw[c][:], in_=k_rows(xT, a)[:, :, t0 : t0 + nv + sum(runs)])
             if c == 0:
                 nc.sync.dma_start(offsets[:], offs)
-        for a in range(PASSES):
+        for a in range(LAST):
             nc.sync.dma_start(out=w_raw[a][:], in_=k_rows(w, a))
+        for m in range(M_TILES):
+            nc.sync.dma_start(out=w_last[m][:], in_=k_rows(w, LAST)[:, :, m * P : (m + 1) * P])
         for m in range(M_TILES):
             if m == 0:
                 for d, pos in enumerate((pos1, pos2, pos3)):
@@ -134,7 +137,7 @@ def tile_picked_sub_lin_relu_sub_e_kernel(tc, xT, w, b, gate, offs, pos1, pos2, 
 
         def round_weights(copy, a, m0, tiles, offset, room=0):
             grouped = placed([P, (tiles + room) * P, PACK], BF16, "w_bf%d_%d" % (a, m0), offset)
-            interleave(copy, grouped[:, 0 : tiles * P, :], w_raw[a][:, :, m0 * P : (m0 + tiles) * P])
+            interleave(copy, grouped[:, 0 : tiles * P, :], w_last[m0][:] if a == LAST else w_raw[a][:, :, m0 * P : (m0 + tiles) * P])
             for m in range(tiles):
                 w_bf[(a, m0 + m)] = grouped[:, m * P : (m + 1) * P, :]
 

@@ -23,14 +23,19 @@ PASSES = K // K_PASS
 LAST = PASSES - 1
 M_TILES = N // P
 HALF = S // 2
+LIST_ROWS = 16
 W_RAW_BYTES = PACK * N * 4
+W_BF_BYTES = P * PACK * 2
 SLOT_NODES = PASSES * N
 SLOT_BYTES = SLOT_NODES * PACK * 2
 
-X_CHUNKS = (
-    [(0, 0, 512, (512,)), (1, 0, 512, (256, 256))]
-    + [(2, 0, 0, (512,)), (2, 512, 128, (256, 128))]
-    + [(LAST, 0, 128, (256, 128)), (LAST, 512, 256, (128, 128))]
+X_LOADS = (
+    (0, ((0, 512), (512, 0))),
+    (1, ((0, 256), (512, 0), (0, 256))),
+    (2, ((0, 256), (0, 256))),
+    (2, ((0, 256), (128, 128))),
+    (3, ((0, 256), (128, 128))),
+    (3, ((0, 128), (256, 0), (0, 128))),
 )
 
 
@@ -53,16 +58,23 @@ def tile_picked_sub_lin_relu_sub_e_kernel(tc, xT, w, b, gate, offs, pos1, pos2, 
         def held(shape, dtype, name):
             return keep.tile(shape, dtype, name=name, align_bytes=64)
 
-        def placed(shape, dtype, name, offset):
-            return slots.tile(shape, dtype, name=name, align_bytes=64, offset=offset)
+        def placed(pool, shape, dtype, name, offset):
+            return pool.tile(shape, dtype, name=name, align_bytes=64, offset=offset)
 
-        offsets = held([P, S // 16], U16, "offsets")
-        places = [held([P, V // 16], U16, "places%d" % d) for d in range(D)]
-        bias = [held([P, 1], F32, "bias0"), after_relu.tile([P, 1], F32, name="bias1", offset=0)]
+        load_nodes = [sum(by_vector + by_scalar for by_vector, by_scalar in runs) for a, runs in X_LOADS]
+        first_node = [sum(load_nodes[:c]) % T for c in range(len(X_LOADS))]
+
+        offsets = held([P, S // LIST_ROWS], U16, "offsets")
+        places = [held([P, V // LIST_ROWS], U16, "places%d" % d) for d in range(D)]
+        bias = [held([P, 1], F32, "bias0"), placed(after_relu, [P, 1], F32, "bias1", 0)]
         gates = [held([P, D, V], F32, "gates%d" % m) for m in range(M_TILES)]
-        x_raw = [held([P, PACK, nv + sum(runs)], F32, "x_raw%d" % c) for c, (a, t0, nv, runs) in enumerate(X_CHUNKS)]
-        w_raw = [raw_w.tile([P, PACK, N], F32, name="w_raw%d" % a, offset=a * W_RAW_BYTES) for a in range(LAST)]
-        w_last = [held([P, PACK, P], F32, "w_last%d" % m) for m in range(M_TILES)]
+        x_raw = [held([P, PACK, n], F32, "x_raw%d" % c) for c, n in enumerate(load_nodes)]
+        w_raw = [placed(raw_w, [P, PACK, N], F32, "w_raw%d" % a, a * W_RAW_BYTES) for a in range(LAST)]
+        w_last_offset = LAST * W_RAW_BYTES
+        w_last = [
+            placed(raw_w, [P, PACK, P], F32, "w_last%d" % m, w_last_offset + m * W_RAW_BYTES // M_TILES)
+            for m in range(M_TILES)
+        ]
         node_words = [held([P, T], U32, "node_words%d" % a) for a in range(PASSES)]
         node_scales = held([P, T], U8, "node_scales")
         picked_scales = held([P, S], U8, "picked_scales")
@@ -78,53 +90,56 @@ def tile_picked_sub_lin_relu_sub_e_kernel(tc, xT, w, b, gate, offs, pos1, pos2, 
         def k_rows(src, a):
             return src[a * K_PASS : (a + 1) * K_PASS, :].rearrange("(p j) c -> p j c", j=PACK)
 
-        for c, (a, t0, nv, runs) in enumerate(X_CHUNKS):
-            nc.sync.dma_start(out=x_raw[c][:], in_=k_rows(xT, a)[:, :, t0 : t0 + nv + sum(runs)])
+        for c, (a, runs) in enumerate(X_LOADS):
+            nc.sync.dma_start(out=x_raw[c][:], in_=k_rows(xT, a)[:, :, first_node[c] : first_node[c] + load_nodes[c]])
             if c == 0:
                 nc.sync.dma_start(offsets[:], offs)
         for a in range(LAST):
             nc.sync.dma_start(out=w_raw[a][:], in_=k_rows(w, a))
         for m in range(M_TILES):
             nc.sync.dma_start(out=w_last[m][:], in_=k_rows(w, LAST)[:, :, m * P : (m + 1) * P])
+        for d, pos in enumerate((pos1, pos2, pos3)):
+            nc.sync.dma_start(places[d][:], pos)
         for m in range(M_TILES):
-            if m == 0:
-                for d, pos in enumerate((pos1, pos2, pos3)):
-                    nc.sync.dma_start(places[d][:], pos)
             nc.sync.dma_start(out=gates[m][:], in_=gate[:, m * P : (m + 1) * P, :].rearrange("d p v -> p d v"))
-
-        def quantize_nodes(a, t0, n, grouped):
-            nc.vector.quantize_mx(
-                out=node_words[a][:, t0 : t0 + n].bitcast(FP8X4),
-                scales=node_scales[PACK * a : P, t0 : t0 + n],
-                in_=grouped[:, 0:n, :].rearrange("p t j -> p (t j)"),
-            )
 
         picked_words = {}
 
         def gather_words(picked, a, j0, j1):
-            nc.vector.tensor_copy(picked[:], node_words[a][:].indirect(offsets[:, j0 // 16 : j1 // 16]))
+            entries = offsets[:, j0 // LIST_ROWS : j1 // LIST_ROWS]
+            nc.vector.tensor_copy(picked[:], node_words[a][:].indirect(entries))
             for h in range(j0 // HALF, j1 // HALF):
                 picked_words[(a, h)] = picked[:, h * HALF - j0 : (h + 1) * HALF - j0]
 
-        slot = 0
-        for c, (a, t0, nv, runs) in enumerate(X_CHUNKS):
-            own = []
-            if nv:
-                by_vector = placed([P, nv, PACK], BF16, "x_bf_vector%d" % c, slot * SLOT_BYTES)
-                interleave(nc.vector.tensor_copy, by_vector[:], x_raw[c][:, :, 0:nv])
-                own.append((0, nv, by_vector))
-            by_scalar = []
-            first = nv
-            for n in runs:
-                slot += 1
-                grouped = placed([P, SLOT_NODES, PACK], BF16, "x_bf_scalar%d" % slot, slot * SLOT_BYTES)
-                interleave(nc.scalar.copy, grouped[:, 0:n, :], x_raw[c][:, :, first : first + n])
-                by_scalar.append((first, n, grouped))
-                first += n
-            runs_ready = by_scalar[:1] + own + by_scalar[1:]
-            for first, n, grouped in runs_ready:
-                quantize_nodes(a, t0 + first, n, grouped)
-            if t0 + nv + sum(runs) == T and a < LAST:
+        fresh_slot = 0
+        scalar_slot = 0
+        for c, (a, runs) in enumerate(X_LOADS):
+            earlier_slot = scalar_slot
+            first = 0
+            for r, (by_vector, by_scalar) in enumerate(runs):
+                nodes = by_vector + by_scalar
+                if by_vector:
+                    slot = earlier_slot
+                else:
+                    fresh_slot += 1
+                    slot = fresh_slot
+                if by_scalar:
+                    scalar_slot = slot
+                room = SLOT_NODES if by_scalar else nodes
+                grouped = placed(slots, [P, room, PACK], BF16, "x_bf%d_%d" % (c, r), slot * SLOT_BYTES)
+                middle = first + by_vector
+                if by_vector:
+                    interleave(nc.vector.tensor_copy, grouped[:, 0:by_vector, :], x_raw[c][:, :, first:middle])
+                if by_scalar:
+                    interleave(nc.scalar.copy, grouped[:, by_vector:nodes, :], x_raw[c][:, :, middle : first + nodes])
+                columns = slice(first_node[c] + first, first_node[c] + first + nodes)
+                nc.vector.quantize_mx(
+                    out=node_words[a][:, columns].bitcast(FP8X4),
+                    scales=node_scales[PACK * a : P, columns],
+                    in_=grouped[:, 0:nodes, :].rearrange("p t j -> p (t j)"),
+                )
+                first += nodes
+            if first_node[c] + load_nodes[c] == T and a < LAST:
                 gather_words(held([P, S], U32, "picked_words%d" % a), a, 0, S)
         nc.vector.tensor_copy(picked_scales[:], node_scales[:].indirect(offsets[:]))
 
@@ -132,22 +147,18 @@ def tile_picked_sub_lin_relu_sub_e_kernel(tc, xT, w, b, gate, offs, pos1, pos2, 
         w_words = {}
         w_scales = {}
 
-        def w_slot(n):
-            return (slot - len(X_CHUNKS[-1][3])) * SLOT_BYTES + n * P * PACK * 2
+        def w_piece(n):
+            return earlier_slot * SLOT_BYTES + n * W_BF_BYTES
 
-        def round_weights(copy, a, m0, tiles, offset, room=0):
-            grouped = placed([P, (tiles + room) * P, PACK], BF16, "w_bf%d_%d" % (a, m0), offset)
-            interleave(copy, grouped[:, 0 : tiles * P, :], w_last[m0][:] if a == LAST else w_raw[a][:, :, m0 * P : (m0 + tiles) * P])
+        def round_weights(copy, a, m0, tiles, piece, spare=0):
+            grouped = placed(slots, [P, (tiles + spare) * P, PACK], BF16, "w_bf%d_%d" % (a, m0), w_piece(piece))
+            raw = w_last[m0][:] if a == LAST else w_raw[a][:, :, m0 * P : (m0 + tiles) * P]
+            interleave(copy, grouped[:, 0 : tiles * P, :], raw)
             for m in range(tiles):
                 w_bf[(a, m0 + m)] = grouped[:, m * P : (m + 1) * P, :]
 
-        def quantize_weights(a, m):
-            name = "%d_%d" % (a, m)
-            words = held([P, P], U32, "w_words" + name)
-            if m == 1 and a < 2:
-                scales = placed([P, P], U8, "w_scales" + name, w_slot(7) + a * P)
-            else:
-                scales = held([P, P], U8, "w_scales" + name)
+        def quantize_weights(a, m, scales):
+            words = held([P, P], U32, "w_words%d_%d" % (a, m))
             nc.vector.quantize_mx(
                 out=words[:].bitcast(FP8X4),
                 scales=scales[:],
@@ -156,36 +167,40 @@ def tile_picked_sub_lin_relu_sub_e_kernel(tc, xT, w, b, gate, offs, pos1, pos2, 
             w_words[(a, m)] = words[:]
             w_scales[(a, m)] = scales[:]
 
-        round_weights(nc.scalar.copy, 0, 0, 2, w_slot(2))
-        round_weights(nc.scalar.copy, 1, 0, 2, w_slot(0))
-        round_weights(nc.scalar.copy, 2, 0, 1, w_slot(4))
-        round_weights(nc.scalar.copy, 3, 0, 1, w_slot(5), room=2)
-        for a in range(PASSES):
-            quantize_weights(a, 0)
-            if a < 2:
-                picked = raw_w.tile([P, HALF], U32, name="picked_last%d" % a, align_bytes=64, offset=a * W_RAW_BYTES)
-                gather_words(picked, LAST, a * HALF, (a + 1) * HALF)
-        round_weights(nc.scalar.copy, 2, 1, 1, w_slot(5))
-        round_weights(nc.vector.tensor_copy, 3, 1, 1, w_slot(6))
-        for a in (0, 1, 3, 2):
-            quantize_weights(a, 1)
+        def free_scales(a, m):
+            return held([P, P], U8, "w_scales%d_%d" % (a, m))
+
+        round_weights(nc.scalar.copy, 0, 0, M_TILES, 2)
+        round_weights(nc.scalar.copy, 1, 0, M_TILES, 0)
+        round_weights(nc.scalar.copy, 2, 0, 1, 4)
+        round_weights(nc.scalar.copy, 3, 0, 1, 5, spare=2)
+        quantize_weights(0, 0, free_scales(0, 0))
+        gather_words(placed(raw_w, [P, HALF], U32, "picked_last0", 0), LAST, 0, HALF)
+        for a in range(1, PASSES):
+            quantize_weights(a, 0, free_scales(a, 0))
+        gather_words(placed(raw_w, [P, HALF], U32, "picked_last1", w_last_offset), LAST, HALF, S)
+        round_weights(nc.scalar.copy, 2, 1, 1, 5)
+        round_weights(nc.vector.tensor_copy, 3, 1, 1, 6)
+        for a in (0, 1):
+            quantize_weights(a, 1, placed(slots, [P, P], U8, "w_scales%d_1" % a, w_piece(7) + a * P))
+        for a in (3, 2):
+            quantize_weights(a, 1, free_scales(a, 1))
 
         def results(m):
-            acc = [psum.tile([P, HALF], F32, name="acc%d" % h) for h in range(2)]
+            acc = [psum.tile([P, HALF], F32, name="acc%d" % h) for h in range(S // HALF)]
             for a in range(PASSES):
-                for h in range(2):
-                    cols = slice(h * HALF, (h + 1) * HALF)
+                for h in range(S // HALF):
                     nc.tensor.matmul_mx(
                         out=acc[h][:],
                         lhsT=w_words[(a, m)].bitcast(FP8X4),
                         lhsT_scale=w_scales[(a, m)],
                         rhs=picked_words[(a, h)].bitcast(FP8X4),
-                        rhs_scale=picked_scales[PACK * a : P, cols],
+                        rhs_scale=picked_scales[PACK * a : P, h * HALF : (h + 1) * HALF],
                         start=(a == 0),
                         stop=(a == LAST),
                     )
             y = held([P, S], F32, "y%d" % m)
-            for h in range(2):
+            for h in range(S // HALF):
                 nc.scalar.activation(out=y[:, h * HALF : (h + 1) * HALF], in_=acc[h][:], func=RELU, bias=bias[m][:])
             return y
 
@@ -194,8 +209,8 @@ def tile_picked_sub_lin_relu_sub_e_kernel(tc, xT, w, b, gate, offs, pos1, pos2, 
             nc.vector.tensor_tensor(product[:], y[:].indirect(places[d][:]), gates[m][:, d, :], MULT)
             return product
 
-        def add(first, second, total):
-            nc.vector.tensor_tensor(total[:], first[:], second[:], ADD)
+        def add(first_term, second_term, total):
+            nc.vector.tensor_tensor(total[:], first_term[:], second_term[:], ADD)
             return total
 
         def store(m, total):
@@ -205,8 +220,8 @@ def tile_picked_sub_lin_relu_sub_e_kernel(tc, xT, w, b, gate, offs, pos1, pos2, 
         y1 = results(1)
         terms0 = [term(0, d, y0) for d in range(D)]
         partial0 = add(terms0[0], terms0[1], held([P, V], F32, "partial0"))
-        first1 = term(1, 0, y1)
-        store(0, add(partial0, terms0[2], after_relu.tile([P, V], F32, name="total0", offset=0)))
-        second1 = term(1, 1, y1)
-        third1 = term(1, 2, y1)
-        store(1, add(add(first1, second1, held([P, V], F32, "partial1")), third1, held([P, V], F32, "total1")))
+        terms1 = [term(1, 0, y1)]
+        store(0, add(partial0, terms0[2], placed(after_relu, [P, V], F32, "total0", 0)))
+        terms1.extend(term(1, d, y1) for d in range(1, D))
+        partial1 = add(terms1[0], terms1[1], held([P, V], F32, "partial1"))
+        store(1, add(partial1, terms1[2], held([P, V], F32, "total1")))

@@ -1,6 +1,7 @@
 from contextlib import ExitStack
 
 import concourse.mybir as mybir
+from concourse.masks import make_identity
 
 K, T, D, S, V, N = 2048, 1024, 3, 512, 256, 256
 FLOPS = 2 * K * N * S
@@ -13,6 +14,7 @@ U16 = mybir.dt.uint16
 U8 = mybir.dt.uint8
 FP8X4 = mybir.dt.float8_e4m3fn_x4
 RELU = mybir.ActivationFunctionType.Relu
+COPY = mybir.ActivationFunctionType.Copy
 MULT = mybir.AluOpType.mult
 ADD = mybir.AluOpType.add
 
@@ -22,27 +24,31 @@ K_PASS = P * PACK
 PASSES = K // K_PASS
 LAST = PASSES - 1
 M_TILES = N // P
+V_TILES = V // P
 HALF = S // 2
 LIST_ROWS = 16
+BANK = 2048
 W_RAW_BYTES = PACK * N * 4
 W_BF_BYTES = P * PACK * 2
 SLOT_NODES = PASSES * N
 SLOT_BYTES = SLOT_NODES * PACK * 2
+WHOLE_W = 2
+RUN = 2
 
+WHOLE = (("scalar", 128), ("vector", 512), ("scalar", 256), ("scalar", 128))
 X_LOADS = (
-    (0, ((0, 512), (512, 0))),
-    (1, ((0, 256), (512, 0), (0, 256))),
-    (2, ((0, 256), (0, 256))),
-    (2, ((0, 256), (128, 128))),
-    (3, ((0, 256), (128, 128))),
-    (3, ((0, 128), (256, 0), (0, 128))),
+    (0, WHOLE),
+    (1, WHOLE),
+    (2, WHOLE),
+    (3, (("scalar", 256), ("vector", 128), ("scalar", 128))),
+    (3, (("scalar", 128), ("vector", 256), ("scalar", 128))),
 )
 
 
 def interleave(copy, grouped, raw):
     copy(
-        out=grouped.rearrange("p (c i) j -> p c j i", i=2),
-        in_=raw.rearrange("p j (c i) -> p c j i", i=2),
+        out=grouped.rearrange("p (c i) j -> p c j i", i=RUN),
+        in_=raw.rearrange("p j (c i) -> p c j i", i=RUN),
     )
 
 
@@ -61,31 +67,42 @@ def tile_picked_sub_lin_relu_sub_e_kernel(tc, xT, w, b, gate, offs, pos1, pos2, 
         def placed(pool, shape, dtype, name, offset):
             return pool.tile(shape, dtype, name=name, align_bytes=64, offset=offset)
 
-        load_nodes = [sum(by_vector + by_scalar for by_vector, by_scalar in runs) for a, runs in X_LOADS]
+        def bank(shape, name, number):
+            return psum.tile(shape, F32, name=name, offset=number * BANK)
+
+        load_nodes = [sum(nodes for engine, nodes in runs) for a, runs in X_LOADS]
         first_node = [sum(load_nodes[:c]) % T for c in range(len(X_LOADS))]
 
         offsets = held([P, S // LIST_ROWS], U16, "offsets")
         places = [held([P, V // LIST_ROWS], U16, "places%d" % d) for d in range(D)]
-        bias = [held([P, 1], F32, "bias0"), placed(after_relu, [P, 1], F32, "bias1", 0)]
-        gates = [held([P, D, V], F32, "gates%d" % m) for m in range(M_TILES)]
+        rows = held([P, V], F32, "rows")
+        identity = held([P, P], F32, "identity")
+        columns = held([P, V_TILES, D + 1], F32, "columns")
+        bias1 = placed(after_relu, [P, 1], F32, "bias1", 0)
+        gates = held([P, D, V], F32, "gates")
         x_raw = [held([P, PACK, n], F32, "x_raw%d" % c) for c, n in enumerate(load_nodes)]
-        w_raw = [placed(raw_w, [P, PACK, N], F32, "w_raw%d" % a, a * W_RAW_BYTES) for a in range(LAST)]
+        w_raw = {}
+        for a in range(WHOLE_W):
+            whole = placed(raw_w, [P, PACK, N], F32, "w_raw%d" % a, a * W_RAW_BYTES)
+            for m in range(M_TILES):
+                w_raw[(a, m)] = whole[:, :, m * P : (m + 1) * P]
+            w_raw[a] = whole
+        for a in range(WHOLE_W, PASSES):
+            room = 3 * PACK if a == LAST else PACK
+            w_raw[(a, 0)] = placed(raw_w, [P, room, P], F32, "w_raw%d_0" % a, a * W_RAW_BYTES)[:, 0:PACK, :]
+            w_raw[(a, 1)] = held([P, PACK, P], F32, "w_raw%d_1" % a)[:]
         w_last_offset = LAST * W_RAW_BYTES
-        w_last = [
-            placed(raw_w, [P, PACK, P], F32, "w_last%d" % m, w_last_offset + m * W_RAW_BYTES // M_TILES)
-            for m in range(M_TILES)
-        ]
         node_words = [held([P, T], U32, "node_words%d" % a) for a in range(PASSES)]
         node_scales = held([P, T], U8, "node_scales")
         picked_scales = held([P, S], U8, "picked_scales")
 
         warm_in = held([P, 8], F32, "warm_in")
         warm_out = held([P, 8], F32, "warm_out")
+        nc.gpsimd.memset(rows[:], 0.0)
+        make_identity(nc, identity[:])
         nc.vector.memset(warm_in[:], 0.0)
         nc.scalar.activation(out=warm_out[:], in_=warm_in[:], func=RELU)
         nc.vector.memset(node_scales[:].bitcast(I32), 0)
-        for m in range(M_TILES):
-            nc.scalar.dma_start(out=bias[m][:], in_=b[m * P : (m + 1) * P, :])
 
         def k_rows(src, a):
             return src[a * K_PASS : (a + 1) * K_PASS, :].rearrange("(p j) c -> p j c", j=PACK)
@@ -94,51 +111,51 @@ def tile_picked_sub_lin_relu_sub_e_kernel(tc, xT, w, b, gate, offs, pos1, pos2, 
             nc.sync.dma_start(out=x_raw[c][:], in_=k_rows(xT, a)[:, :, first_node[c] : first_node[c] + load_nodes[c]])
             if c == 0:
                 nc.sync.dma_start(offsets[:], offs)
-        for a in range(LAST):
+                nc.sync.dma_start(out=rows[0:D, :], in_=gate[:, 0, :])
+                nc.sync.dma_start(out=rows[D : D + 1, :], in_=b.rearrange("n o -> o n"))
+        for a in range(WHOLE_W):
             nc.sync.dma_start(out=w_raw[a][:], in_=k_rows(w, a))
         for m in range(M_TILES):
-            nc.sync.dma_start(out=w_last[m][:], in_=k_rows(w, LAST)[:, :, m * P : (m + 1) * P])
+            for a in range(WHOLE_W, PASSES):
+                nc.sync.dma_start(out=w_raw[(a, m)], in_=k_rows(w, a)[:, :, m * P : (m + 1) * P])
         for d, pos in enumerate((pos1, pos2, pos3)):
             nc.sync.dma_start(places[d][:], pos)
-        for m in range(M_TILES):
-            nc.sync.dma_start(out=gates[m][:], in_=gate[:, m * P : (m + 1) * P, :].rearrange("d p v -> p d v"))
+        nc.sync.dma_start(out=gates[:], in_=gate[:, P:N, :].rearrange("d p v -> p d v"))
+
+        turned_rows = bank([P, V_TILES, P], "turned_rows", 3)
+        for h in range(V_TILES):
+            nc.tensor.transpose(turned_rows[:, h, :], rows[:, h * P : (h + 1) * P], identity[:])
+        nc.scalar.copy(out=columns[:], in_=turned_rows[:, :, 0 : D + 1])
+        nc.scalar.copy(out=bias1[:, 0:1], in_=turned_rows[:, 1, D : D + 1])
+        bias = [columns[:, 0, D : D + 1], bias1[:, 0:1]]
 
         picked_words = {}
 
         def gather_words(picked, a, j0, j1):
             entries = offsets[:, j0 // LIST_ROWS : j1 // LIST_ROWS]
-            nc.vector.tensor_copy(picked[:], node_words[a][:].indirect(entries))
-            for h in range(j0 // HALF, j1 // HALF):
-                picked_words[(a, h)] = picked[:, h * HALF - j0 : (h + 1) * HALF - j0]
+            nc.vector.tensor_copy(picked[:, j0:j1], node_words[a][:].indirect(entries))
+            picked_words[a] = picked
 
-        fresh_slot = 0
-        scalar_slot = 0
+        slot = 0
         for c, (a, runs) in enumerate(X_LOADS):
-            earlier_slot = scalar_slot
             first = 0
-            for r, (by_vector, by_scalar) in enumerate(runs):
-                nodes = by_vector + by_scalar
-                if by_vector:
-                    slot = earlier_slot
-                else:
-                    fresh_slot += 1
-                    slot = fresh_slot
-                if by_scalar:
-                    scalar_slot = slot
-                room = SLOT_NODES if by_scalar else nodes
-                grouped = placed(slots, [P, room, PACK], BF16, "x_bf%d_%d" % (c, r), slot * SLOT_BYTES)
-                middle = first + by_vector
-                if by_vector:
-                    interleave(nc.vector.tensor_copy, grouped[:, 0:by_vector, :], x_raw[c][:, :, first:middle])
-                if by_scalar:
-                    interleave(nc.scalar.copy, grouped[:, by_vector:nodes, :], x_raw[c][:, :, middle : first + nodes])
-                columns = slice(first_node[c] + first, first_node[c] + first + nodes)
-                nc.vector.quantize_mx(
-                    out=node_words[a][:, columns].bitcast(FP8X4),
-                    scales=node_scales[PACK * a : P, columns],
-                    in_=grouped[:, 0:nodes, :].rearrange("p t j -> p (t j)"),
-                )
+            rounded = []
+            for r, (engine, nodes) in enumerate(runs):
+                copy = nc.vector.tensor_copy if engine == "vector" else nc.scalar.copy
+                room = nodes
+                if (c, r) == (len(X_LOADS) - 1, 0):
+                    room, opening_slot = SLOT_NODES, slot
+                grouped = placed(slots, [P, room, PACK], BF16, "x_bf%d_%d" % (c, r), slot)
+                slot += room * PACK * 2
+                interleave(copy, grouped[:, 0:nodes, :], x_raw[c][:, :, first : first + nodes])
+                rounded.append((grouped[:, 0:nodes, :], slice(first_node[c] + first, first_node[c] + first + nodes)))
                 first += nodes
+            for grouped, span in rounded:
+                nc.vector.quantize_mx(
+                    out=node_words[a][:, span].bitcast(FP8X4),
+                    scales=node_scales[PACK * a : P, span],
+                    in_=grouped.rearrange("p t j -> p (t j)"),
+                )
             if first_node[c] + load_nodes[c] == T and a < LAST:
                 gather_words(held([P, S], U32, "picked_words%d" % a), a, 0, S)
         nc.vector.tensor_copy(picked_scales[:], node_scales[:].indirect(offsets[:]))
@@ -147,18 +164,18 @@ def tile_picked_sub_lin_relu_sub_e_kernel(tc, xT, w, b, gate, offs, pos1, pos2, 
         w_words = {}
         w_scales = {}
 
-        def w_piece(n):
-            return earlier_slot * SLOT_BYTES + n * W_BF_BYTES
-
-        def round_weights(copy, a, m0, tiles, piece, spare=0):
-            grouped = placed(slots, [P, (tiles + spare) * P, PACK], BF16, "w_bf%d_%d" % (a, m0), w_piece(piece))
-            raw = w_last[m0][:] if a == LAST else w_raw[a][:, :, m0 * P : (m0 + tiles) * P]
-            interleave(copy, grouped[:, 0 : tiles * P, :], raw)
+        def round_weights(copy, a, m0, tiles, pool, offset):
+            grouped = placed(pool, [P, tiles * P, PACK], BF16, "w_bf%d_%d" % (a, m0), offset)
+            interleave(copy, grouped[:], w_raw[a][:] if tiles == M_TILES else w_raw[(a, m0)])
             for m in range(tiles):
                 w_bf[(a, m0 + m)] = grouped[:, m * P : (m + 1) * P, :]
 
-        def quantize_weights(a, m, scales):
+        def quantize_weights(a, m):
             words = held([P, P], U32, "w_words%d_%d" % (a, m))
+            if m == 0:
+                scales = held([P, P], U8, "w_scales%d_0" % a)
+            else:
+                scales = placed(raw_w, [P, P], U8, "w_scales%d_1" % a, late_piece(4) + a * P)
             nc.vector.quantize_mx(
                 out=words[:].bitcast(FP8X4),
                 scales=scales[:],
@@ -167,61 +184,98 @@ def tile_picked_sub_lin_relu_sub_e_kernel(tc, xT, w, b, gate, offs, pos1, pos2, 
             w_words[(a, m)] = words[:]
             w_scales[(a, m)] = scales[:]
 
-        def free_scales(a, m):
-            return held([P, P], U8, "w_scales%d_%d" % (a, m))
+        def w_piece(n):
+            return opening_slot + n * W_BF_BYTES
 
-        round_weights(nc.scalar.copy, 0, 0, M_TILES, 2)
-        round_weights(nc.scalar.copy, 1, 0, M_TILES, 0)
-        round_weights(nc.scalar.copy, 2, 0, 1, 4)
-        round_weights(nc.scalar.copy, 3, 0, 1, 5, spare=2)
-        quantize_weights(0, 0, free_scales(0, 0))
-        gather_words(placed(raw_w, [P, HALF], U32, "picked_last0", 0), LAST, 0, HALF)
+        def late_piece(n):
+            return w_last_offset + n * W_BF_BYTES
+
+        round_weights(nc.scalar.copy, 0, 0, M_TILES, slots, w_piece(0))
         for a in range(1, PASSES):
-            quantize_weights(a, 0, free_scales(a, 0))
-        gather_words(placed(raw_w, [P, HALF], U32, "picked_last1", w_last_offset), LAST, HALF, S)
-        round_weights(nc.scalar.copy, 2, 1, 1, 5)
-        round_weights(nc.vector.tensor_copy, 3, 1, 1, 6)
-        for a in (0, 1):
-            quantize_weights(a, 1, placed(slots, [P, P], U8, "w_scales%d_1" % a, w_piece(7) + a * P))
-        for a in (3, 2):
-            quantize_weights(a, 1, free_scales(a, 1))
+            round_weights(nc.scalar.copy, a, 0, 1, slots, w_piece(1 + a))
+        for a in range(1, LAST):
+            round_weights(nc.scalar.copy, a, 1, 1, raw_w, late_piece(a - 1))
+        picked_last = [placed(raw_w, [P, HALF], U32, "picked_last0", 0), placed(raw_w, [P, HALF], U32, "picked_last1", 2 * W_RAW_BYTES)]
 
-        def results(m):
-            acc = [psum.tile([P, HALF], F32, name="acc%d" % h) for h in range(S // HALF)]
+        def gather_last(h):
+            entries = offsets[:, h * HALF // LIST_ROWS : (h + 1) * HALF // LIST_ROWS]
+            nc.vector.tensor_copy(picked_last[h][:], node_words[LAST][:].indirect(entries))
+
+        quantize_weights(0, 0)
+        gather_last(0)
+        quantize_weights(1, 0)
+        quantize_weights(2, 0)
+        gather_last(1)
+        quantize_weights(3, 0)
+        quantize_weights(0, 1)
+        round_weights(nc.vector.tensor_copy, LAST, 1, 1, raw_w, late_piece(2))
+        for a in range(1, PASSES):
+            quantize_weights(a, 1)
+
+        acc = {(m, h): bank([P, HALF], "acc%d_%d" % (m, h), (0, 1, 2, 7)[2 * m + h]) for m in range(M_TILES) for h in range(2)}
+
+        def multiply(m, a):
+            for h in range(2):
+                span = slice(h * HALF, (h + 1) * HALF)
+                nc.tensor.matmul_mx(
+                    out=acc[(m, h)][:],
+                    lhsT=w_words[(a, m)].bitcast(FP8X4),
+                    lhsT_scale=w_scales[(a, m)],
+                    rhs=(picked_last[h][:] if a == LAST else picked_words[a][:, span]).bitcast(FP8X4),
+                    rhs_scale=picked_scales[PACK * a : P, span],
+                    start=(a == 0),
+                    stop=(a == LAST),
+                )
+
+        for m in range(M_TILES):
             for a in range(PASSES):
-                for h in range(S // HALF):
-                    nc.tensor.matmul_mx(
-                        out=acc[h][:],
-                        lhsT=w_words[(a, m)].bitcast(FP8X4),
-                        lhsT_scale=w_scales[(a, m)],
-                        rhs=picked_words[(a, h)].bitcast(FP8X4),
-                        rhs_scale=picked_scales[PACK * a : P, h * HALF : (h + 1) * HALF],
-                        start=(a == 0),
-                        stop=(a == LAST),
-                    )
-            y = held([P, S], F32, "y%d" % m)
-            for h in range(S // HALF):
-                nc.scalar.activation(out=y[:, h * HALF : (h + 1) * HALF], in_=acc[h][:], func=RELU, bias=bias[m][:])
-            return y
+                multiply(m, a)
+        y = []
+        for m in range(M_TILES):
+            y.append(held([P, S], F32, "y%d" % m))
+            for h in range(2):
+                nc.scalar.activation(out=y[m][:, h * HALF : (h + 1) * HALF], in_=acc[(m, h)][:], func=RELU, bias=bias[m])
 
-        def term(m, d, y):
-            product = held([P, V], F32, "term%d_%d" % (m, d))
-            nc.vector.tensor_tensor(product[:], y[:].indirect(places[d][:]), gates[m][:, d, :], MULT)
-            return product
+        scaled = placed(after_relu, [P, D, V], F32, "scaled", 0)
+        sums = [bank([P, P], "sum%d" % h, h) for h in range(V_TILES)]
+        for d in range(D):
+            fetched = held([P, V], F32, "fetched%d" % d)
+            nc.vector.tensor_copy(fetched[:], y[0][:].indirect(places[d][:]))
+            turned = bank([P, V], "turned%d" % d, 3 + d)
+            for h in range(V_TILES):
+                nc.tensor.transpose(turned[:, h * P : (h + 1) * P], fetched[:, h * P : (h + 1) * P], identity[:])
+            for h in range(V_TILES):
+                nc.scalar.activation(
+                    out=scaled[:, d, h * P : (h + 1) * P],
+                    in_=turned[:, h * P : (h + 1) * P],
+                    func=COPY,
+                    scale=columns[:, h, d : d + 1],
+                )
+        for d in range(D):
+            for h in range(V_TILES):
+                nc.tensor.matmul(
+                    sums[h][:],
+                    scaled[:, d, h * P : (h + 1) * P],
+                    identity[:],
+                    start=(d == 0),
+                    stop=(d == D - 1),
+                    is_transpose=True,
+                )
+        total0 = held([P, V], F32, "total0")
+        for h in range(V_TILES):
+            nc.scalar.copy(out=total0[:, h * P : (h + 1) * P], in_=sums[h][:])
+        nc.sync.dma_start(out=out[0:P, :], in_=total0[:])
 
-        def add(first_term, second_term, total):
-            nc.vector.tensor_tensor(total[:], first_term[:], second_term[:], ADD)
-            return total
-
-        def store(m, total):
-            nc.sync.dma_start(out=out[m * P : (m + 1) * P, :], in_=total[:])
-
-        y0 = results(0)
-        y1 = results(1)
-        terms0 = [term(0, d, y0) for d in range(D)]
-        partial0 = add(terms0[0], terms0[1], held([P, V], F32, "partial0"))
-        terms1 = [term(1, 0, y1)]
-        store(0, add(partial0, terms0[2], placed(after_relu, [P, V], F32, "total0", 0)))
-        terms1.extend(term(1, d, y1) for d in range(1, D))
-        partial1 = add(terms1[0], terms1[1], held([P, V], F32, "partial1"))
-        store(1, add(partial1, terms1[2], held([P, V], F32, "total1")))
+        products = []
+        for d in range(D):
+            products.append(held([P, V], F32, "product%d" % d))
+            nc.vector.tensor_tensor(products[d][:], y[1][:].indirect(places[d][:]), gates[:, d, :], MULT)
+        partial = held([P, V], F32, "partial")
+        total1 = held([P, V], F32, "total1")
+        for h in range(V_TILES):
+            span = slice(h * P, (h + 1) * P)
+            nc.vector.tensor_tensor(partial[:, span], products[0][:, span], products[1][:, span], ADD)
+        for h in range(V_TILES):
+            span = slice(h * P, (h + 1) * P)
+            nc.vector.tensor_tensor(total1[:, span], partial[:, span], products[2][:, span], ADD)
+        nc.sync.dma_start(out=out[P:N, :], in_=total1[:])

@@ -96,12 +96,8 @@ def tile_picked_sub_lin_relu_sub_e_kernel(tc, xT, w, b, gate, offs, pos1, pos2, 
         node_scales = held([P, T], U8, "node_scales")
         picked_scales = held([P, S], U8, "picked_scales")
 
-        warm_in = held([P, 8], F32, "warm_in")
-        warm_out = held([P, 8], F32, "warm_out")
         nc.gpsimd.memset(rows[:], 0.0)
         make_identity(nc, identity[:])
-        nc.vector.memset(warm_in[:], 0.0)
-        nc.scalar.activation(out=warm_out[:], in_=warm_in[:], func=RELU)
         nc.vector.memset(node_scales[:].bitcast(I32), 0)
 
         def k_rows(src, a):

@@ -107,10 +107,11 @@ def tile_picked_sub_lin_relu_sub_e_kernel(tc, xT, w, b, gate, offs, pos1, pos2, 
             nc.sync.dma_start(out=x_raw[c][:], in_=k_rows(xT, a)[:, :, first_node[c] : first_node[c] + load_nodes[c]])
             if c == 0:
                 nc.sync.dma_start(offsets[:], offs)
-                nc.sync.dma_start(out=rows[0:D, :], in_=gate[:, 0, :])
-                nc.sync.dma_start(out=rows[D : D + 1, :], in_=b.rearrange("n o -> o n"))
         for a in range(WHOLE_W):
             nc.sync.dma_start(out=w_raw[a][:], in_=k_rows(w, a))
+            if a == 0:
+                nc.sync.dma_start(out=rows[0:D, :], in_=gate[:, 0, :])
+                nc.sync.dma_start(out=rows[D : D + 1, :], in_=b.rearrange("n o -> o n"))
         for m in range(M_TILES):
             for a in range(WHOLE_W, PASSES):
                 nc.sync.dma_start(out=w_raw[(a, m)], in_=k_rows(w, a)[:, :, m * P : (m + 1) * P])

@@ -8,7 +8,6 @@ FLOPS = 2 * K * N * S
 
 F32 = mybir.dt.float32
 BF16 = mybir.dt.bfloat16
-I32 = mybir.dt.int32
 U32 = mybir.dt.uint32
 U16 = mybir.dt.uint16
 U8 = mybir.dt.uint8
@@ -17,6 +16,7 @@ RELU = mybir.ActivationFunctionType.Relu
 COPY = mybir.ActivationFunctionType.Copy
 MULT = mybir.AluOpType.mult
 ADD = mybir.AluOpType.add
+MAX = mybir.AluOpType.max
 
 P = 128
 PACK = 4
@@ -28,21 +28,11 @@ V_TILES = V // P
 HALF = S // 2
 LIST_ROWS = 16
 BANK = 2048
-W_RAW_BYTES = PACK * N * 4
-W_BF_BYTES = P * PACK * 2
-SLOT_NODES = PASSES * N
-SLOT_BYTES = SLOT_NODES * PACK * 2
-WHOLE_W = 2
 RUN = 2
-
-WHOLE = (("scalar", 128), ("vector", 512), ("scalar", 256), ("scalar", 128))
-X_LOADS = (
-    (0, WHOLE),
-    (1, WHOLE),
-    (2, WHOLE),
-    (3, (("scalar", 256), ("vector", 128), ("scalar", 128))),
-    (3, (("scalar", 128), ("vector", 256), ("scalar", 128))),
-)
+X_LOADS = ((2, 2), (2, 2), (2, 2), (2, 1, 1))
+SLOT = HALF * PACK * 2
+RAW3 = 5 * SLOT
+W_BF_AT = {(0, 0): 0, (0, 1): SLOT, (1, 0): 2 * SLOT, (2, 0): 3 * SLOT, (2, 1): 3 * SLOT, (3, 0): 4 * SLOT, (1, 1): RAW3}
 
 
 def interleave(copy, grouped, raw):
@@ -56,191 +46,189 @@ def tile_picked_sub_lin_relu_sub_e_kernel(tc, xT, w, b, gate, offs, pos1, pos2, 
     nc = tc.nc
     with ExitStack() as ctx:
         keep = ctx.enter_context(tc.tile_pool(name="keep", bufs=1))
-        slots = ctx.enter_context(tc.tile_pool(name="slots", bufs=1))
-        raw_w = ctx.enter_context(tc.tile_pool(name="raw_w", bufs=1))
-        after_relu = ctx.enter_context(tc.tile_pool(name="after_relu", bufs=1))
+        order = ctx.enter_context(tc.tile_pool(name="order", bufs=1))
         psum = ctx.enter_context(tc.psum_pool(name="psum", bufs=1))
 
         def held(shape, dtype, name):
             return keep.tile(shape, dtype, name=name, align_bytes=64)
 
-        def placed(pool, shape, dtype, name, offset):
-            return pool.tile(shape, dtype, name=name, align_bytes=64, offset=offset)
+        def placed(shape, dtype, name, offset):
+            return order.tile(shape, dtype, name=name, align_bytes=64, offset=offset)
 
         def bank(shape, name, number):
             return psum.tile(shape, F32, name=name, offset=number * BANK)
 
-        load_nodes = [sum(nodes for engine, nodes in runs) for a, runs in X_LOADS]
-        first_node = [sum(load_nodes[:c]) % T for c in range(len(X_LOADS))]
+        def k_rows(src, a):
+            return src[a * K_PASS : (a + 1) * K_PASS, :].rearrange("(p j) c -> p j c", j=PACK)
 
         offsets = held([P, S // LIST_ROWS], U16, "offsets")
         places = [held([P, V // LIST_ROWS], U16, "places%d" % d) for d in range(D)]
         rows = held([P, V], F32, "rows")
         identity = held([P, P], F32, "identity")
         columns = held([P, V_TILES, D + 1], F32, "columns")
-        bias1 = placed(after_relu, [P, 1], F32, "bias1", 0)
         gates = held([P, D, V], F32, "gates")
-        x_raw = [held([P, PACK, n], F32, "x_raw%d" % c) for c, n in enumerate(load_nodes)]
-        w_raw = {}
-        for a in range(WHOLE_W):
-            whole = placed(raw_w, [P, PACK, N], F32, "w_raw%d" % a, a * W_RAW_BYTES)
-            for m in range(M_TILES):
-                w_raw[(a, m)] = whole[:, :, m * P : (m + 1) * P]
-            w_raw[a] = whole
-        for a in range(WHOLE_W, PASSES):
-            room = 3 * PACK if a == LAST else PACK
-            w_raw[(a, 0)] = placed(raw_w, [P, room, P], F32, "w_raw%d_0" % a, a * W_RAW_BYTES)[:, 0:PACK, :]
-            w_raw[(a, 1)] = held([P, PACK, P], F32, "w_raw%d_1" % a)[:]
-        w_last_offset = LAST * W_RAW_BYTES
-        node_words = [held([P, T], U32, "node_words%d" % a) for a in range(PASSES)]
-        node_scales = held([P, T], U8, "node_scales")
-        picked_scales = held([P, S], U8, "picked_scales")
+        w_whole = [held([P, PACK, N], F32, "w_raw%d" % a) for a in range(LAST)]
+        w_last = [placed([P, PACK, P], F32, "w_raw3_0", RAW3), held([P, PACK, P], F32, "w_raw3_1")]
+        w_raw = {(a, m): w_whole[a][:, :, m * P : (m + 1) * P] for a in range(LAST) for m in range(M_TILES)}
+        for m in range(M_TILES):
+            w_raw[(LAST, m)] = w_last[m][:]
 
         nc.gpsimd.memset(rows[:], 0.0)
         make_identity(nc, identity[:])
-        nc.vector.memset(node_scales[:].bitcast(I32), 0)
 
-        def k_rows(src, a):
-            return src[a * K_PASS : (a + 1) * K_PASS, :].rearrange("(p j) c -> p j c", j=PACK)
+        plane = {}
 
-        for c, (a, runs) in enumerate(X_LOADS):
-            nc.sync.dma_start(out=x_raw[c][:], in_=k_rows(xT, a)[:, :, first_node[c] : first_node[c] + load_nodes[c]])
-            if c == 0:
-                nc.sync.dma_start(offsets[:], offs)
-        for a in range(WHOLE_W):
-            nc.sync.dma_start(out=w_raw[a][:], in_=k_rows(w, a))
-            if a == 0:
-                nc.sync.dma_start(out=rows[0:D, :], in_=gate[:, 0, :])
-                nc.sync.dma_start(out=rows[D : D + 1, :], in_=b.rearrange("n o -> o n"))
-        for m in range(M_TILES):
-            for a in range(WHOLE_W, PASSES):
-                nc.sync.dma_start(out=w_raw[(a, m)], in_=k_rows(w, a)[:, :, m * P : (m + 1) * P])
-        for d, pos in enumerate((pos1, pos2, pos3)):
-            nc.sync.dma_start(places[d][:], pos)
+        def load_x(a):
+            j0 = 0
+            for count in X_LOADS[a]:
+                raw = held([P, count, T], F32, "x_raw%d_%d" % (a, j0))
+                nc.sync.dma_start(out=raw[:], in_=k_rows(xT, a)[:, j0 : j0 + count, :])
+                if (a, j0) == (0, 0):
+                    nc.sync.dma_start(offsets[:], offs)
+                    nc.sync.dma_start(out=rows[0:D, :], in_=gate[:, 0, :])
+                    nc.sync.dma_start(out=rows[D : D + 1, :], in_=b.rearrange("n o -> o n"))
+                for j in range(count):
+                    plane[(a, j0 + j)] = raw[:, j, :]
+                j0 += count
+
+        for a in range(PASSES):
+            load_x(a)
+        for a in range(LAST):
+            nc.sync.dma_start(out=w_whole[a][:], in_=k_rows(w, a))
+        nc.sync.dma_start(out=w_last[0][:], in_=k_rows(w, LAST)[:, :, 0:P])
+        nc.sync.dma_start(places[1][:], pos2)
+        nc.sync.dma_start(out=w_last[1][:], in_=k_rows(w, LAST)[:, :, P:N])
+        nc.sync.dma_start(places[0][:], pos1)
+        nc.sync.dma_start(places[2][:], pos3)
         nc.sync.dma_start(out=gates[:], in_=gate[:, P:N, :].rearrange("d p v -> p d v"))
 
         turned_rows = bank([P, V_TILES, P], "turned_rows", 3)
         for h in range(V_TILES):
             nc.tensor.transpose(turned_rows[:, h, :], rows[:, h * P : (h + 1) * P], identity[:])
         nc.scalar.copy(out=columns[:], in_=turned_rows[:, :, 0 : D + 1])
-        nc.scalar.copy(out=bias1[:, 0:1], in_=turned_rows[:, 1, D : D + 1])
-        bias = [columns[:, 0, D : D + 1], bias1[:, 0:1]]
+        bias = [columns[:, m, D : D + 1] for m in range(M_TILES)]
 
-        picked_words = {}
+        def gather(engine, dst, window, entries):
+            if engine == "vector":
+                nc.vector.tensor_copy(dst, window.indirect(entries))
+            else:
+                nc.scalar.activation(dst, window.indirect(entries), COPY)
 
-        def gather_words(picked, a, j0, j1):
-            entries = offsets[:, j0 // LIST_ROWS : j1 // LIST_ROWS]
-            nc.vector.tensor_copy(picked[:, j0:j1], node_words[a][:].indirect(entries))
-            picked_words[a] = picked
+        def entries(j0, j1):
+            return offsets[:, j0 // LIST_ROWS : j1 // LIST_ROWS]
 
-        slot = 0
-        for c, (a, runs) in enumerate(X_LOADS):
-            first = 0
-            rounded = []
-            for r, (engine, nodes) in enumerate(runs):
-                copy = nc.vector.tensor_copy if engine == "vector" else nc.scalar.copy
-                room = nodes
-                if (c, r) == (len(X_LOADS) - 1, 0):
-                    room, opening_slot = SLOT_NODES, slot
-                grouped = placed(slots, [P, room, PACK], BF16, "x_bf%d_%d" % (c, r), slot)
-                slot += room * PACK * 2
-                interleave(copy, grouped[:, 0:nodes, :], x_raw[c][:, :, first : first + nodes])
-                rounded.append((grouped[:, 0:nodes, :], slice(first_node[c] + first, first_node[c] + first + nodes)))
-                first += nodes
-            for grouped, span in rounded:
-                nc.vector.quantize_mx(
-                    out=node_words[a][:, span].bitcast(FP8X4),
-                    scales=node_scales[PACK * a : P, span],
-                    in_=grouped.rearrange("p t j -> p (t j)"),
-                )
-            if first_node[c] + load_nodes[c] == T and a < LAST:
-                gather_words(held([P, S], U32, "picked_words%d" % a), a, 0, S)
-        nc.vector.tensor_copy(picked_scales[:], node_scales[:].indirect(offsets[:]))
+        def quantize(name, grouped, columns, offset=None):
+            if offset is None:
+                words = held([P, columns], U32, name + "_words")
+            else:
+                words = placed([P, columns], U32, name + "_words", offset)
+            scales = held([P, columns], U8, name + "_scales")
+            nc.vector.quantize_mx(out=words[:].bitcast(FP8X4), scales=scales[:], in_=grouped.rearrange("p c j -> p (c j)"))
+            return words, scales
+
+        x_q = {}
+        w_q = {}
+
+        def pick(a, engines):
+            picked = held([P, PACK, S], F32, "picked%d" % a)
+            for j in range(PACK):
+                if engines[j] == "both":
+                    gather("scalar", picked[:, j, 0:HALF], plane[(a, j)], entries(0, HALF))
+                    gather("vector", picked[:, j, HALF:S], plane[(a, j)], entries(HALF, S))
+                else:
+                    gather(engines[j], picked[:, j, :], plane[(a, j)], offsets[:])
+            return picked
+
+        def x_pass(a, engines):
+            picked = pick(a, engines)
+            grouped = held([P, S, PACK], BF16, "x_bf%d" % a)
+            interleave(nc.vector.tensor_copy, grouped[:], picked[:])
+            words, scales = quantize("x%d" % a, grouped[:], S)
+            for h in range(2):
+                x_q[(a, h)] = (words[:, h * HALF : (h + 1) * HALF], scales[:, h * HALF : (h + 1) * HALF])
+
+        x_pass(0, ("vector", "scalar", "vector", "scalar"))
+        x_pass(1, ("scalar", "scalar", "vector", "scalar"))
+        x_pass(2, ("scalar", "scalar", "vector", "scalar"))
+
+        picked_last = pick(LAST, ("scalar", "both", "both", "both"))
+        x_bf = {}
+
+        def round_x(h):
+            if h == 1:
+                x_bf[h] = placed([P, HALF, PACK], BF16, "x_bf_last1", 0)
+            else:
+                x_bf[h] = held([P, HALF, PACK], BF16, "x_bf_last0")
+            interleave(nc.vector.tensor_copy, x_bf[h][:], picked_last[:, :, h * HALF : (h + 1) * HALF])
 
         w_bf = {}
-        w_words = {}
-        w_scales = {}
 
-        def round_weights(copy, a, m0, tiles, pool, offset):
-            grouped = placed(pool, [P, tiles * P, PACK], BF16, "w_bf%d_%d" % (a, m0), offset)
-            interleave(copy, grouped[:], w_raw[a][:] if tiles == M_TILES else w_raw[(a, m0)])
-            for m in range(tiles):
-                w_bf[(a, m0 + m)] = grouped[:, m * P : (m + 1) * P, :]
-
-        def quantize_weights(a, m):
-            words = held([P, P], U32, "w_words%d_%d" % (a, m))
-            if m == 0:
-                scales = held([P, P], U8, "w_scales%d_0" % a)
+        def round_w(copy, a, m):
+            if (a, m) in W_BF_AT:
+                w_bf[(a, m)] = placed([P, P, PACK], BF16, "w_bf%d_%d" % (a, m), W_BF_AT[(a, m)])
             else:
-                scales = placed(raw_w, [P, P], U8, "w_scales%d_1" % a, late_piece(4) + a * P)
-            nc.vector.quantize_mx(
-                out=words[:].bitcast(FP8X4),
-                scales=scales[:],
-                in_=w_bf[(a, m)].rearrange("p c j -> p (c j)"),
-            )
-            w_words[(a, m)] = words[:]
-            w_scales[(a, m)] = scales[:]
+                w_bf[(a, m)] = held([P, P, PACK], BF16, "w_bf%d_%d" % (a, m))
+            interleave(copy, w_bf[(a, m)][:], w_raw[(a, m)])
 
-        def w_piece(n):
-            return opening_slot + n * W_BF_BYTES
+        def quantize_w(a, m):
+            words, scales = quantize("w%d_%d" % (a, m), w_bf[(a, m)][:], P, 4 * SLOT if (a, m) == (2, 1) else None)
+            w_q[(a, m)] = (words[:], scales[:])
 
-        def late_piece(n):
-            return w_last_offset + n * W_BF_BYTES
+        def quantize_x(h):
+            words, scales = quantize("x_last%d" % h, x_bf[h][:], HALF, (1 + h) * SLOT)
+            x_q[(LAST, h)] = (words[:], scales[:])
 
-        round_weights(nc.scalar.copy, 0, 0, M_TILES, slots, w_piece(0))
-        for a in range(1, PASSES):
-            round_weights(nc.scalar.copy, a, 0, 1, slots, w_piece(1 + a))
-        for a in range(1, LAST):
-            round_weights(nc.scalar.copy, a, 1, 1, raw_w, late_piece(a - 1))
-        picked_last = [placed(raw_w, [P, HALF], U32, "picked_last0", 0), placed(raw_w, [P, HALF], U32, "picked_last1", 2 * W_RAW_BYTES)]
-
-        def gather_last(h):
-            entries = offsets[:, h * HALF // LIST_ROWS : (h + 1) * HALF // LIST_ROWS]
-            nc.vector.tensor_copy(picked_last[h][:], node_words[LAST][:].indirect(entries))
-
-        quantize_weights(0, 0)
-        gather_last(0)
-        quantize_weights(1, 0)
-        quantize_weights(2, 0)
-        gather_last(1)
-        quantize_weights(3, 0)
-        quantize_weights(0, 1)
-        round_weights(nc.vector.tensor_copy, LAST, 1, 1, raw_w, late_piece(2))
-        for a in range(1, PASSES):
-            quantize_weights(a, 1)
+        for a, m in ((0, 0), (0, 1), (1, 0), (2, 0), (3, 0), (1, 1)):
+            round_w(nc.scalar.copy, a, m)
+        round_x(0)
+        quantize_w(0, 0)
+        round_x(1)
+        quantize_w(0, 1)
+        quantize_x(0)
+        quantize_w(1, 0)
+        quantize_x(1)
+        quantize_w(2, 0)
+        round_w(nc.vector.tensor_copy, 2, 1)
+        quantize_w(3, 0)
+        quantize_w(2, 1)
+        round_w(nc.vector.tensor_copy, 3, 1)
+        quantize_w(1, 1)
+        quantize_w(3, 1)
 
         acc = {(m, h): bank([P, HALF], "acc%d_%d" % (m, h), (0, 1, 2, 7)[2 * m + h]) for m in range(M_TILES) for h in range(2)}
 
-        def multiply(m, a):
+        def multiply(a, m):
             for h in range(2):
-                span = slice(h * HALF, (h + 1) * HALF)
                 nc.tensor.matmul_mx(
                     out=acc[(m, h)][:],
-                    lhsT=w_words[(a, m)].bitcast(FP8X4),
-                    lhsT_scale=w_scales[(a, m)],
-                    rhs=(picked_last[h][:] if a == LAST else picked_words[a][:, span]).bitcast(FP8X4),
-                    rhs_scale=picked_scales[PACK * a : P, span],
+                    lhsT=w_q[(a, m)][0].bitcast(FP8X4),
+                    lhsT_scale=w_q[(a, m)][1],
+                    rhs=x_q[(a, h)][0].bitcast(FP8X4),
+                    rhs_scale=x_q[(a, h)][1],
                     start=(a == 0),
                     stop=(a == LAST),
                 )
 
-        for m in range(M_TILES):
-            for a in range(PASSES):
-                multiply(m, a)
-        y = []
-        for m in range(M_TILES):
-            y.append(held([P, S], F32, "y%d" % m))
-            for h in range(2):
-                nc.scalar.activation(out=y[m][:, h * HALF : (h + 1) * HALF], in_=acc[(m, h)][:], func=RELU, bias=bias[m])
+        for a, m in ((0, 0), (0, 1), (1, 0), (2, 0), (3, 0), (2, 1), (1, 1), (3, 1)):
+            multiply(a, m)
 
-        scaled = placed(after_relu, [P, D, V], F32, "scaled", 0)
+        y = [held([P, S], F32, "y%d" % m) for m in range(M_TILES)]
+        fetched = [held([P, V], F32, "fetched%d" % d) for d in range(D)]
+        fetched_last = held([P, V], F32, "fetched_last")
+        nc.scalar.activation(out=y[0][:, 0:HALF], in_=acc[(0, 0)][:], func=RELU, bias=bias[0])
+        nc.vector.tensor_scalar(y[0][:, HALF:S], acc[(0, 1)][:], bias[0], 0.0, ADD, MAX)
+        for d in range(D):
+            gather("scalar" if d == 1 else "vector", fetched[d][:], y[0][:], places[d][:])
+        for h in range(2):
+            nc.scalar.activation(out=y[1][:, h * HALF : (h + 1) * HALF], in_=acc[(1, h)][:], func=RELU, bias=bias[1])
+        gather("scalar", fetched_last[:], y[1][:], places[D - 1][:])
+
+        scaled = held([P, D, V], F32, "scaled")
         sums = [bank([P, P], "sum%d" % h, h) for h in range(V_TILES)]
         for d in range(D):
-            fetched = held([P, V], F32, "fetched%d" % d)
-            nc.vector.tensor_copy(fetched[:], y[0][:].indirect(places[d][:]))
             turned = bank([P, V], "turned%d" % d, 3 + d)
             for h in range(V_TILES):
-                nc.tensor.transpose(turned[:, h * P : (h + 1) * P], fetched[:, h * P : (h + 1) * P], identity[:])
+                nc.tensor.transpose(turned[:, h * P : (h + 1) * P], fetched[d][:, h * P : (h + 1) * P], identity[:])
             for h in range(V_TILES):
                 nc.scalar.activation(
                     out=scaled[:, d, h * P : (h + 1) * P],
@@ -266,12 +254,11 @@ def tile_picked_sub_lin_relu_sub_e_kernel(tc, xT, w, b, gate, offs, pos1, pos2, 
         products = []
         for d in range(D):
             products.append(held([P, V], F32, "product%d" % d))
-            nc.vector.tensor_tensor(products[d][:], y[1][:].indirect(places[d][:]), gates[:, d, :], MULT)
+            source = fetched_last[:] if d == D - 1 else y[1][:].indirect(places[d][:])
+            nc.vector.tensor_tensor(products[d][:], source, gates[:, d, :], MULT)
         partial = held([P, V], F32, "partial")
         total1 = held([P, V], F32, "total1")
-        for h in range(V_TILES):
-            span = slice(h * P, (h + 1) * P)
-            nc.vector.tensor_tensor(partial[:, span], products[0][:, span], products[1][:, span], ADD)
+        nc.vector.tensor_tensor(partial[:], products[0][:], products[1][:], ADD)
         for h in range(V_TILES):
             span = slice(h * P, (h + 1) * P)
             nc.vector.tensor_tensor(total1[:, span], partial[:, span], products[2][:, span], ADD)

@@ -32,6 +32,7 @@ RUN = 2
 X_LOADS = ((2, 2), (2, 2), (2, 2), (2, 1, 1))
 SLOT = HALF * PACK * 2
 RAW3 = 5 * SLOT
+COLUMNS = 6 * SLOT
 W_BF_AT = {(0, 0): 0, (0, 1): SLOT, (1, 0): 2 * SLOT, (2, 0): 3 * SLOT, (2, 1): 3 * SLOT, (3, 0): 4 * SLOT, (1, 1): RAW3}
 
 
@@ -65,7 +66,7 @@ def tile_picked_sub_lin_relu_sub_e_kernel(tc, xT, w, b, gate, offs, pos1, pos2, 
         places = [held([P, V // LIST_ROWS], U16, "places%d" % d) for d in range(D)]
         rows = held([P, V], F32, "rows")
         identity = held([P, P], F32, "identity")
-        columns = held([P, V_TILES, D + 1], F32, "columns")
+        columns = placed([P, V_TILES, D + 1], F32, "columns", COLUMNS)
         gates = held([P, D, V], F32, "gates")
         w_whole = [held([P, PACK, N], F32, "w_raw%d" % a) for a in range(LAST)]
         w_last = [placed([P, PACK, P], F32, "w_raw3_0", RAW3), held([P, PACK, P], F32, "w_raw3_1")]
@@ -214,14 +215,12 @@ def tile_picked_sub_lin_relu_sub_e_kernel(tc, xT, w, b, gate, offs, pos1, pos2, 
 
         y = [held([P, S], F32, "y%d" % m) for m in range(M_TILES)]
         fetched = [held([P, V], F32, "fetched%d" % d) for d in range(D)]
-        fetched_last = held([P, V], F32, "fetched_last")
         nc.scalar.activation(out=y[0][:, 0:HALF], in_=acc[(0, 0)][:], func=RELU, bias=bias[0])
         nc.vector.tensor_scalar(y[0][:, HALF:S], acc[(0, 1)][:], bias[0], 0.0, ADD, MAX)
         for d in range(D):
             gather("scalar" if d == 1 else "vector", fetched[d][:], y[0][:], places[d][:])
         for h in range(2):
             nc.scalar.activation(out=y[1][:, h * HALF : (h + 1) * HALF], in_=acc[(1, h)][:], func=RELU, bias=bias[1])
-        gather("scalar", fetched_last[:], y[1][:], places[D - 1][:])
 
         scaled = held([P, D, V], F32, "scaled")
         sums = [bank([P, P], "sum%d" % h, h) for h in range(V_TILES)]
@@ -236,6 +235,9 @@ def tile_picked_sub_lin_relu_sub_e_kernel(tc, xT, w, b, gate, offs, pos1, pos2, 
                     func=COPY,
                     scale=columns[:, h, d : d + 1],
                 )
+        fetched_last = placed([P, V], F32, "fetched_last", COLUMNS)
+        for h in range(V_TILES):
+            gather("scalar", fetched_last[:, h * P : (h + 1) * P], y[1][:], places[D - 1][:, h * P // LIST_ROWS : (h + 1) * P // LIST_ROWS])
         for d in range(D):
             for h in range(V_TILES):
                 nc.tensor.matmul(
@@ -251,15 +253,15 @@ def tile_picked_sub_lin_relu_sub_e_kernel(tc, xT, w, b, gate, offs, pos1, pos2, 
             nc.scalar.copy(out=total0[:, h * P : (h + 1) * P], in_=sums[h][:])
         nc.sync.dma_start(out=out[0:P, :], in_=total0[:])
 
-        products = []
-        for d in range(D):
-            products.append(held([P, V], F32, "product%d" % d))
-            source = fetched_last[:] if d == D - 1 else y[1][:].indirect(places[d][:])
-            nc.vector.tensor_tensor(products[d][:], source, gates[:, d, :], MULT)
+        products = [held([P, V], F32, "product%d" % d) for d in range(D)]
+        for d in range(D - 1):
+            nc.vector.tensor_tensor(products[d][:], y[1][:].indirect(places[d][:]), gates[:, d, :], MULT)
         partial = held([P, V], F32, "partial")
         total1 = held([P, V], F32, "total1")
+        spans = [slice(h * P, (h + 1) * P) for h in range(V_TILES)]
+        nc.vector.tensor_tensor(products[2][:, spans[0]], fetched_last[:, spans[0]], gates[:, 2, spans[0]], MULT)
         nc.vector.tensor_tensor(partial[:], products[0][:], products[1][:], ADD)
-        for h in range(V_TILES):
-            span = slice(h * P, (h + 1) * P)
+        nc.vector.tensor_tensor(products[2][:, spans[1]], fetched_last[:, spans[1]], gates[:, 2, spans[1]], MULT)
+        for span in spans:
             nc.vector.tensor_tensor(total1[:, span], partial[:, span], products[2][:, span], ADD)
         nc.sync.dma_start(out=out[P:N, :], in_=total1[:])

@@ -29,7 +29,7 @@ HALF = S // 2
 LIST_ROWS = 16
 BANK = 2048
 RUN = 2
-X_LOADS = ((2, 2), (2, 2), (2, 2), (2, 1, 1))
+X_LOADS = ((2, 2), (2, 2), (2, 1, 1), (2, 1, 1))
 SLOT = HALF * PACK * 2
 RAW3 = 5 * SLOT
 COLUMNS = 6 * SLOT
@@ -66,7 +66,7 @@ def tile_picked_sub_lin_relu_sub_e_kernel(tc, xT, w, b, gate, offs, pos1, pos2, 
         places = [held([P, V // LIST_ROWS], U16, "places%d" % d) for d in range(D)]
         rows = held([P, V], F32, "rows")
         identity = held([P, P], F32, "identity")
-        columns = placed([P, V_TILES, D + 1], F32, "columns", COLUMNS)
+        columns = [placed([P, D + 1], F32, "columns0", COLUMNS), held([P, D + 1], F32, "columns1")]
         gates = held([P, D, V], F32, "gates")
         w_whole = [held([P, PACK, N], F32, "w_raw%d" % a) for a in range(LAST)]
         w_last = [placed([P, PACK, P], F32, "w_raw3_0", RAW3), held([P, PACK, P], F32, "w_raw3_1")]
@@ -106,8 +106,9 @@ def tile_picked_sub_lin_relu_sub_e_kernel(tc, xT, w, b, gate, offs, pos1, pos2, 
         turned_rows = bank([P, V_TILES, P], "turned_rows", 3)
         for h in range(V_TILES):
             nc.tensor.transpose(turned_rows[:, h, :], rows[:, h * P : (h + 1) * P], identity[:])
-        nc.scalar.copy(out=columns[:], in_=turned_rows[:, :, 0 : D + 1])
-        bias = [columns[:, m, D : D + 1] for m in range(M_TILES)]
+        for h in range(V_TILES):
+            nc.scalar.copy(out=columns[h][:], in_=turned_rows[:, h, 0 : D + 1])
+        bias = [columns[m][:, D : D + 1] for m in range(M_TILES)]
 
         def gather(engine, dst, window, entries):
             if engine == "vector":
@@ -150,7 +151,7 @@ def tile_picked_sub_lin_relu_sub_e_kernel(tc, xT, w, b, gate, offs, pos1, pos2, 
 
         x_pass(0, ("vector", "scalar", "vector", "scalar"))
         x_pass(1, ("scalar", "scalar", "vector", "scalar"))
-        x_pass(2, ("scalar", "scalar", "vector", "scalar"))
+        x_pass(2, ("scalar", "scalar", "vector", "both"))
 
         picked_last = pick(LAST, ("scalar", "both", "both", "both"))
         x_bf = {}
@@ -233,7 +234,7 @@ def tile_picked_sub_lin_relu_sub_e_kernel(tc, xT, w, b, gate, offs, pos1, pos2, 
                     out=scaled[:, d, h * P : (h + 1) * P],
                     in_=turned[:, h * P : (h + 1) * P],
                     func=COPY,
-                    scale=columns[:, h, d : d + 1],
+                    scale=columns[h][:, d : d + 1],
                 )
         fetched_last = placed([P, V], F32, "fetched_last", COLUMNS)
         for h in range(V_TILES):

@@ -29,11 +29,25 @@ HALF = S // 2
 LIST_ROWS = 16
 BANK = 2048
 RUN = 2
-X_LOADS = ((2, 2), (2, 2), (2, 1, 1), (2, 1, 1))
-SLOT = HALF * PACK * 2
-RAW3 = 5 * SLOT
-COLUMNS = 6 * SLOT
-W_BF_AT = {(0, 0): 0, (0, 1): SLOT, (1, 0): 2 * SLOT, (2, 0): 3 * SLOT, (2, 1): 3 * SLOT, (3, 0): 4 * SLOT, (1, 1): RAW3}
+
+X_LOADS = ((2, 2), (2, 2), (2, 2), (2, 1, 1))
+GATHERED_BY = (
+    ("vector", "scalar", "vector", "scalar"),
+    ("scalar", "scalar", "vector", "scalar"),
+    ("scalar", "scalar", "vector", "scalar"),
+    ("scalar", "both", "both", "both"),
+)
+
+W_BF_BYTES = P * PACK * 2
+X_BF_BYTES = HALF * PACK * 2
+AFTER_FIRST_W = 0
+AFTER_LAST_W = 2 * X_BF_BYTES
+AFTER_SCALING = 4 * X_BF_BYTES
+W_BF_AT = {(0, 0): AFTER_FIRST_W, (1, 1): AFTER_LAST_W, (LAST, 1): AFTER_LAST_W + W_BF_BYTES}
+W_WORDS_AT = {(2, 1): AFTER_LAST_W + 2 * W_BF_BYTES}
+
+ACC_BANK = (0, 1, 2, 7)
+TURN_BANK = 3
 
 
 def interleave(copy, grouped, raw):
@@ -62,123 +76,115 @@ def tile_picked_sub_lin_relu_sub_e_kernel(tc, xT, w, b, gate, offs, pos1, pos2, 
         def k_rows(src, a):
             return src[a * K_PASS : (a + 1) * K_PASS, :].rearrange("(p j) c -> p j c", j=PACK)
 
+        def entries(table, first, stop):
+            return table[:, first // LIST_ROWS : stop // LIST_ROWS]
+
         offsets = held([P, S // LIST_ROWS], U16, "offsets")
         places = [held([P, V // LIST_ROWS], U16, "places%d" % d) for d in range(D)]
         rows = held([P, V], F32, "rows")
         identity = held([P, P], F32, "identity")
-        columns = [placed([P, D + 1], F32, "columns0", COLUMNS), held([P, D + 1], F32, "columns1")]
+        columns = [placed([P, D + 1], F32, "columns0", AFTER_SCALING), held([P, D + 1], F32, "columns1")]
         gates = held([P, D, V], F32, "gates")
         w_whole = [held([P, PACK, N], F32, "w_raw%d" % a) for a in range(LAST)]
-        w_last = [placed([P, PACK, P], F32, "w_raw3_0", RAW3), held([P, PACK, P], F32, "w_raw3_1")]
+        w_last = [placed([P, PACK + 1, P], F32, "w_raw3_0", AFTER_LAST_W)[:, 0:PACK, :], held([P, PACK, P], F32, "w_raw3_1")[:]]
         w_raw = {(a, m): w_whole[a][:, :, m * P : (m + 1) * P] for a in range(LAST) for m in range(M_TILES)}
         for m in range(M_TILES):
-            w_raw[(LAST, m)] = w_last[m][:]
+            w_raw[(LAST, m)] = w_last[m]
 
         nc.gpsimd.memset(rows[:], 0.0)
         make_identity(nc, identity[:])
 
         plane = {}
-
-        def load_x(a):
-            j0 = 0
+        for a in range(PASSES):
+            first = 0
             for count in X_LOADS[a]:
-                raw = held([P, count, T], F32, "x_raw%d_%d" % (a, j0))
-                nc.sync.dma_start(out=raw[:], in_=k_rows(xT, a)[:, j0 : j0 + count, :])
-                if (a, j0) == (0, 0):
+                raw = held([P, count, T], F32, "x_raw%d_%d" % (a, first))
+                nc.sync.dma_start(out=raw[:], in_=k_rows(xT, a)[:, first : first + count, :])
+                if (a, first) == (0, 0):
                     nc.sync.dma_start(offsets[:], offs)
                     nc.sync.dma_start(out=rows[0:D, :], in_=gate[:, 0, :])
                     nc.sync.dma_start(out=rows[D : D + 1, :], in_=b.rearrange("n o -> o n"))
                 for j in range(count):
-                    plane[(a, j0 + j)] = raw[:, j, :]
-                j0 += count
-
-        for a in range(PASSES):
-            load_x(a)
+                    plane[(a, first + j)] = raw[:, j, :]
+                first += count
         for a in range(LAST):
             nc.sync.dma_start(out=w_whole[a][:], in_=k_rows(w, a))
-        nc.sync.dma_start(out=w_last[0][:], in_=k_rows(w, LAST)[:, :, 0:P])
+        nc.sync.dma_start(out=w_last[0], in_=k_rows(w, LAST)[:, :, 0:P])
         nc.sync.dma_start(places[1][:], pos2)
-        nc.sync.dma_start(out=w_last[1][:], in_=k_rows(w, LAST)[:, :, P:N])
+        nc.sync.dma_start(out=w_last[1], in_=k_rows(w, LAST)[:, :, P:N])
         nc.sync.dma_start(places[0][:], pos1)
         nc.sync.dma_start(places[2][:], pos3)
         nc.sync.dma_start(out=gates[:], in_=gate[:, P:N, :].rearrange("d p v -> p d v"))
 
-        turned_rows = bank([P, V_TILES, P], "turned_rows", 3)
+        turned_rows = bank([P, V_TILES, P], "turned_rows", TURN_BANK)
         for h in range(V_TILES):
             nc.tensor.transpose(turned_rows[:, h, :], rows[:, h * P : (h + 1) * P], identity[:])
         for h in range(V_TILES):
             nc.scalar.copy(out=columns[h][:], in_=turned_rows[:, h, 0 : D + 1])
         bias = [columns[m][:, D : D + 1] for m in range(M_TILES)]
 
-        def gather(engine, dst, window, entries):
+        def gather(engine, dst, window, picks):
             if engine == "vector":
-                nc.vector.tensor_copy(dst, window.indirect(entries))
+                nc.vector.tensor_copy(dst, window.indirect(picks))
             else:
-                nc.scalar.activation(dst, window.indirect(entries), COPY)
+                nc.scalar.activation(dst, window.indirect(picks), COPY)
 
-        def entries(j0, j1):
-            return offsets[:, j0 // LIST_ROWS : j1 // LIST_ROWS]
-
-        def quantize(name, grouped, columns, offset=None):
+        def quantize(name, grouped, width, offset=None):
             if offset is None:
-                words = held([P, columns], U32, name + "_words")
+                words = held([P, width], U32, name + "_words")
             else:
-                words = placed([P, columns], U32, name + "_words", offset)
-            scales = held([P, columns], U8, name + "_scales")
+                words = placed([P, width], U32, name + "_words", offset)
+            scales = held([P, width], U8, name + "_scales")
             nc.vector.quantize_mx(out=words[:].bitcast(FP8X4), scales=scales[:], in_=grouped.rearrange("p c j -> p (c j)"))
             return words, scales
 
-        x_q = {}
-        w_q = {}
-
-        def pick(a, engines):
+        def pick(a):
             picked = held([P, PACK, S], F32, "picked%d" % a)
-            for j in range(PACK):
-                if engines[j] == "both":
-                    gather("scalar", picked[:, j, 0:HALF], plane[(a, j)], entries(0, HALF))
-                    gather("vector", picked[:, j, HALF:S], plane[(a, j)], entries(HALF, S))
+            for j, engine in enumerate(GATHERED_BY[a]):
+                if engine == "both":
+                    gather("scalar", picked[:, j, 0:HALF], plane[(a, j)], entries(offsets, 0, HALF))
+                    gather("vector", picked[:, j, HALF:S], plane[(a, j)], entries(offsets, HALF, S))
                 else:
-                    gather(engines[j], picked[:, j, :], plane[(a, j)], offsets[:])
+                    gather(engine, picked[:, j, :], plane[(a, j)], offsets[:])
             return picked
 
-        def x_pass(a, engines):
-            picked = pick(a, engines)
+        x_q = {}
+        for a in range(LAST):
+            picked = pick(a)
             grouped = held([P, S, PACK], BF16, "x_bf%d" % a)
             interleave(nc.vector.tensor_copy, grouped[:], picked[:])
             words, scales = quantize("x%d" % a, grouped[:], S)
             for h in range(2):
                 x_q[(a, h)] = (words[:, h * HALF : (h + 1) * HALF], scales[:, h * HALF : (h + 1) * HALF])
 
-        x_pass(0, ("vector", "scalar", "vector", "scalar"))
-        x_pass(1, ("scalar", "scalar", "vector", "scalar"))
-        x_pass(2, ("scalar", "scalar", "vector", "both"))
-
-        picked_last = pick(LAST, ("scalar", "both", "both", "both"))
+        picked_last = pick(LAST)
         x_bf = {}
 
         def round_x(h):
             if h == 1:
-                x_bf[h] = placed([P, HALF, PACK], BF16, "x_bf_last1", 0)
+                x_bf[h] = placed([P, HALF, PACK], BF16, "x_bf_last1", AFTER_FIRST_W)
             else:
                 x_bf[h] = held([P, HALF, PACK], BF16, "x_bf_last0")
             interleave(nc.vector.tensor_copy, x_bf[h][:], picked_last[:, :, h * HALF : (h + 1) * HALF])
 
+        def quantize_x(h):
+            words, scales = quantize("x_last%d" % h, x_bf[h][:], HALF, AFTER_FIRST_W + X_BF_BYTES if h == 0 else None)
+            x_q[(LAST, h)] = (words[:], scales[:])
+
         w_bf = {}
+        w_q = {}
 
         def round_w(copy, a, m):
             if (a, m) in W_BF_AT:
-                w_bf[(a, m)] = placed([P, P, PACK], BF16, "w_bf%d_%d" % (a, m), W_BF_AT[(a, m)])
+                room = 3 * P if (a, m) == (0, 0) else P
+                w_bf[(a, m)] = placed([P, room, PACK], BF16, "w_bf%d_%d" % (a, m), W_BF_AT[(a, m)])[:, 0:P, :]
             else:
-                w_bf[(a, m)] = held([P, P, PACK], BF16, "w_bf%d_%d" % (a, m))
-            interleave(copy, w_bf[(a, m)][:], w_raw[(a, m)])
+                w_bf[(a, m)] = held([P, P, PACK], BF16, "w_bf%d_%d" % (a, m))[:]
+            interleave(copy, w_bf[(a, m)], w_raw[(a, m)])
 
         def quantize_w(a, m):
-            words, scales = quantize("w%d_%d" % (a, m), w_bf[(a, m)][:], P, 4 * SLOT if (a, m) == (2, 1) else None)
+            words, scales = quantize("w%d_%d" % (a, m), w_bf[(a, m)], P, W_WORDS_AT.get((a, m)))
             w_q[(a, m)] = (words[:], scales[:])
-
-        def quantize_x(h):
-            words, scales = quantize("x_last%d" % h, x_bf[h][:], HALF, (1 + h) * SLOT)
-            x_q[(LAST, h)] = (words[:], scales[:])
 
         for a, m in ((0, 0), (0, 1), (1, 0), (2, 0), (3, 0), (1, 1)):
             round_w(nc.scalar.copy, a, m)
@@ -189,17 +195,16 @@ def tile_picked_sub_lin_relu_sub_e_kernel(tc, xT, w, b, gate, offs, pos1, pos2, 
         quantize_x(0)
         quantize_w(1, 0)
         quantize_x(1)
-        quantize_w(2, 0)
         round_w(nc.vector.tensor_copy, 2, 1)
+        quantize_w(2, 0)
         quantize_w(3, 0)
         quantize_w(2, 1)
         round_w(nc.vector.tensor_copy, 3, 1)
         quantize_w(1, 1)
         quantize_w(3, 1)
 
-        acc = {(m, h): bank([P, HALF], "acc%d_%d" % (m, h), (0, 1, 2, 7)[2 * m + h]) for m in range(M_TILES) for h in range(2)}
-
-        def multiply(a, m):
+        acc = {(m, h): bank([P, HALF], "acc%d_%d" % (m, h), ACC_BANK[2 * m + h]) for m in range(M_TILES) for h in range(2)}
+        for a, m in ((0, 0), (0, 1), (1, 0), (2, 0), (3, 0), (2, 1), (1, 1), (3, 1)):
             for h in range(2):
                 nc.tensor.matmul_mx(
                     out=acc[(m, h)][:],
@@ -211,47 +216,33 @@ def tile_picked_sub_lin_relu_sub_e_kernel(tc, xT, w, b, gate, offs, pos1, pos2, 
                     stop=(a == LAST),
                 )
 
-        for a, m in ((0, 0), (0, 1), (1, 0), (2, 0), (3, 0), (2, 1), (1, 1), (3, 1)):
-            multiply(a, m)
-
         y = [held([P, S], F32, "y%d" % m) for m in range(M_TILES)]
         fetched = [held([P, V], F32, "fetched%d" % d) for d in range(D)]
         nc.scalar.activation(out=y[0][:, 0:HALF], in_=acc[(0, 0)][:], func=RELU, bias=bias[0])
         nc.vector.tensor_scalar(y[0][:, HALF:S], acc[(0, 1)][:], bias[0], 0.0, ADD, MAX)
-        for d in range(D):
-            gather("scalar" if d == 1 else "vector", fetched[d][:], y[0][:], places[d][:])
+        for d, engine in enumerate(("vector", "scalar", "vector")):
+            gather(engine, fetched[d][:], y[0][:], places[d][:])
         for h in range(2):
             nc.scalar.activation(out=y[1][:, h * HALF : (h + 1) * HALF], in_=acc[(1, h)][:], func=RELU, bias=bias[1])
 
+        spans = [slice(h * P, (h + 1) * P) for h in range(V_TILES)]
         scaled = held([P, D, V], F32, "scaled")
-        sums = [bank([P, P], "sum%d" % h, h) for h in range(V_TILES)]
+        sums = [bank([P, P], "sum%d" % h, ACC_BANK[h]) for h in range(V_TILES)]
         for d in range(D):
-            turned = bank([P, V], "turned%d" % d, 3 + d)
-            for h in range(V_TILES):
-                nc.tensor.transpose(turned[:, h * P : (h + 1) * P], fetched[d][:, h * P : (h + 1) * P], identity[:])
-            for h in range(V_TILES):
-                nc.scalar.activation(
-                    out=scaled[:, d, h * P : (h + 1) * P],
-                    in_=turned[:, h * P : (h + 1) * P],
-                    func=COPY,
-                    scale=columns[h][:, d : d + 1],
-                )
-        fetched_last = placed([P, V], F32, "fetched_last", COLUMNS)
-        for h in range(V_TILES):
-            gather("scalar", fetched_last[:, h * P : (h + 1) * P], y[1][:], places[D - 1][:, h * P // LIST_ROWS : (h + 1) * P // LIST_ROWS])
+            turned = bank([P, V], "turned%d" % d, TURN_BANK + d)
+            for span in spans:
+                nc.tensor.transpose(turned[:, span], fetched[d][:, span], identity[:])
+            for h, span in enumerate(spans):
+                nc.scalar.activation(out=scaled[:, d, span], in_=turned[:, span], func=COPY, scale=columns[h][:, d : d + 1])
+        fetched_last = placed([P, V], F32, "fetched_last", AFTER_SCALING)
+        for span in spans:
+            gather("scalar", fetched_last[:, span], y[1][:], entries(places[D - 1], span.start, span.stop))
         for d in range(D):
-            for h in range(V_TILES):
-                nc.tensor.matmul(
-                    sums[h][:],
-                    scaled[:, d, h * P : (h + 1) * P],
-                    identity[:],
-                    start=(d == 0),
-                    stop=(d == D - 1),
-                    is_transpose=True,
-                )
+            for h, span in enumerate(spans):
+                nc.tensor.matmul(sums[h][:], scaled[:, d, span], identity[:], start=(d == 0), stop=(d == D - 1), is_transpose=True)
         total0 = held([P, V], F32, "total0")
-        for h in range(V_TILES):
-            nc.scalar.copy(out=total0[:, h * P : (h + 1) * P], in_=sums[h][:])
+        for h, span in enumerate(spans):
+            nc.scalar.copy(out=total0[:, span], in_=sums[h][:])
         nc.sync.dma_start(out=out[0:P, :], in_=total0[:])
 
         products = [held([P, V], F32, "product%d" % d) for d in range(D)]
@@ -259,10 +250,9 @@ def tile_picked_sub_lin_relu_sub_e_kernel(tc, xT, w, b, gate, offs, pos1, pos2, 
             nc.vector.tensor_tensor(products[d][:], y[1][:].indirect(places[d][:]), gates[:, d, :], MULT)
         partial = held([P, V], F32, "partial")
         total1 = held([P, V], F32, "total1")
-        spans = [slice(h * P, (h + 1) * P) for h in range(V_TILES)]
-        nc.vector.tensor_tensor(products[2][:, spans[0]], fetched_last[:, spans[0]], gates[:, 2, spans[0]], MULT)
+        nc.vector.tensor_tensor(products[D - 1][:, spans[0]], fetched_last[:, spans[0]], gates[:, D - 1, spans[0]], MULT)
         nc.vector.tensor_tensor(partial[:], products[0][:], products[1][:], ADD)
-        nc.vector.tensor_tensor(products[2][:, spans[1]], fetched_last[:, spans[1]], gates[:, 2, spans[1]], MULT)
+        nc.vector.tensor_tensor(products[D - 1][:, spans[1]], fetched_last[:, spans[1]], gates[:, D - 1, spans[1]], MULT)
         for span in spans:
-            nc.vector.tensor_tensor(total1[:, span], partial[:, span], products[2][:, span], ADD)
+            nc.vector.tensor_tensor(total1[:, span], partial[:, span], products[D - 1][:, span], ADD)
         nc.sync.dma_start(out=out[P:N, :], in_=total1[:])

@@ -16,7 +16,6 @@ RELU = mybir.ActivationFunctionType.Relu
 COPY = mybir.ActivationFunctionType.Copy
 MULT = mybir.AluOpType.mult
 ADD = mybir.AluOpType.add
-MAX = mybir.AluOpType.max
 
 P = 128
 PACK = 4
@@ -38,16 +37,7 @@ GATHERED_BY = (
     ("scalar", "both", "both", "both"),
 )
 
-W_BF_BYTES = P * PACK * 2
-X_BF_BYTES = HALF * PACK * 2
-AFTER_FIRST_W = 0
-AFTER_LAST_W = 2 * X_BF_BYTES
-AFTER_SCALING = 4 * X_BF_BYTES
-W_BF_AT = {(0, 0): AFTER_FIRST_W, (1, 1): AFTER_LAST_W, (LAST, 1): AFTER_LAST_W + W_BF_BYTES}
-W_WORDS_AT = {(2, 1): AFTER_LAST_W + 2 * W_BF_BYTES}
-
-ACC_BANK = (0, 1, 2, 7)
-TURN_BANK = 3
+W_RAW_BYTES = PACK * P * 4
 
 
 def interleave(copy, grouped, raw):
@@ -83,13 +73,13 @@ def tile_picked_sub_lin_relu_sub_e_kernel(tc, xT, w, b, gate, offs, pos1, pos2, 
         places = [held([P, V // LIST_ROWS], U16, "places%d" % d) for d in range(D)]
         rows = held([P, V], F32, "rows")
         identity = held([P, P], F32, "identity")
-        columns = [placed([P, D + 1], F32, "columns0", AFTER_SCALING), held([P, D + 1], F32, "columns1")]
+        columns = held([P, V_TILES, D + 1], F32, "columns")
         gates = held([P, D, V], F32, "gates")
-        w_whole = [held([P, PACK, N], F32, "w_raw%d" % a) for a in range(LAST)]
-        w_last = [placed([P, PACK + 1, P], F32, "w_raw3_0", AFTER_LAST_W)[:, 0:PACK, :], held([P, PACK, P], F32, "w_raw3_1")[:]]
-        w_raw = {(a, m): w_whole[a][:, :, m * P : (m + 1) * P] for a in range(LAST) for m in range(M_TILES)}
-        for m in range(M_TILES):
-            w_raw[(LAST, m)] = w_last[m]
+        w_raw = {
+            (a, m): placed([P, PACK, P], F32, "w_raw%d_%d" % (a, m), (m * PASSES + a) * W_RAW_BYTES)
+            for m in range(M_TILES)
+            for a in range(PASSES)
+        }
 
         nc.gpsimd.memset(rows[:], 0.0)
         make_identity(nc, identity[:])
@@ -107,21 +97,29 @@ def tile_picked_sub_lin_relu_sub_e_kernel(tc, xT, w, b, gate, offs, pos1, pos2, 
                 for j in range(count):
                     plane[(a, first + j)] = raw[:, j, :]
                 first += count
-        for a in range(LAST):
-            nc.sync.dma_start(out=w_whole[a][:], in_=k_rows(w, a))
-        nc.sync.dma_start(out=w_last[0], in_=k_rows(w, LAST)[:, :, 0:P])
-        nc.sync.dma_start(places[1][:], pos2)
-        nc.sync.dma_start(out=w_last[1], in_=k_rows(w, LAST)[:, :, P:N])
-        nc.sync.dma_start(places[0][:], pos1)
-        nc.sync.dma_start(places[2][:], pos3)
-        nc.sync.dma_start(out=gates[:], in_=gate[:, P:N, :].rearrange("d p v -> p d v"))
 
-        turned_rows = bank([P, V_TILES, P], "turned_rows", TURN_BANK)
+        def load_w(a, m):
+            nc.sync.dma_start(out=w_raw[(a, m)][:], in_=k_rows(w, a)[:, :, m * P : (m + 1) * P])
+
+        for a in range(PASSES):
+            load_w(a, 0)
+        for a in range(LAST):
+            load_w(a, 1)
+        nc.sync.dma_start(places[0][:], pos1)
+        load_w(LAST, 1)
+        nc.sync.dma_start(places[2][:], pos3)
+        nc.sync.dma_start(places[1][:], pos2)
+
+        turned_rows = bank([P, V_TILES, P], "turned_rows", 4)
         for h in range(V_TILES):
             nc.tensor.transpose(turned_rows[:, h, :], rows[:, h * P : (h + 1) * P], identity[:])
-        for h in range(V_TILES):
-            nc.scalar.copy(out=columns[h][:], in_=turned_rows[:, h, 0 : D + 1])
-        bias = [columns[m][:, D : D + 1] for m in range(M_TILES)]
+        nc.scalar.copy(out=columns[:], in_=turned_rows[:, :, 0 : D + 1])
+        bias = [columns[:, m, D : D + 1] for m in range(M_TILES)]
+        for d in range(D):
+            spread = bank([P, V], "spread%d" % d, 5 + d)
+            for h in range(V_TILES):
+                nc.tensor.transpose(spread[:, h * P : (h + 1) * P], columns[:, h, d : d + 1].to_broadcast([P, P]), identity[:])
+            nc.vector.tensor_copy(out=gates[:, d, :], in_=spread[:])
 
         def gather(engine, dst, window, picks):
             if engine == "vector":
@@ -160,99 +158,78 @@ def tile_picked_sub_lin_relu_sub_e_kernel(tc, xT, w, b, gate, offs, pos1, pos2, 
         picked_last = pick(LAST)
         x_bf = {}
 
-        def round_x(h):
-            if h == 1:
-                x_bf[h] = placed([P, HALF, PACK], BF16, "x_bf_last1", AFTER_FIRST_W)
-            else:
-                x_bf[h] = held([P, HALF, PACK], BF16, "x_bf_last0")
-            interleave(nc.vector.tensor_copy, x_bf[h][:], picked_last[:, :, h * HALF : (h + 1) * HALF])
+        def round_x(h, grouped):
+            x_bf[h] = grouped
+            interleave(nc.vector.tensor_copy, grouped[:], picked_last[:, :, h * HALF : (h + 1) * HALF])
 
         def quantize_x(h):
-            words, scales = quantize("x_last%d" % h, x_bf[h][:], HALF, AFTER_FIRST_W + X_BF_BYTES if h == 0 else None)
+            words, scales = quantize("x_last%d" % h, x_bf[h][:], HALF, W_RAW_BYTES if h == 0 else None)
             x_q[(LAST, h)] = (words[:], scales[:])
 
         w_bf = {}
         w_q = {}
 
         def round_w(copy, a, m):
-            if (a, m) in W_BF_AT:
-                room = 3 * P if (a, m) == (0, 0) else P
-                w_bf[(a, m)] = placed([P, room, PACK], BF16, "w_bf%d_%d" % (a, m), W_BF_AT[(a, m)])[:, 0:P, :]
-            else:
-                w_bf[(a, m)] = held([P, P, PACK], BF16, "w_bf%d_%d" % (a, m))[:]
-            interleave(copy, w_bf[(a, m)], w_raw[(a, m)])
+            w_bf[(a, m)] = held([P, P, PACK], BF16, "w_bf%d_%d" % (a, m))
+            interleave(copy, w_bf[(a, m)][:], w_raw[(a, m)][:])
 
         def quantize_w(a, m):
-            words, scales = quantize("w%d_%d" % (a, m), w_bf[(a, m)], P, W_WORDS_AT.get((a, m)))
+            words, scales = quantize("w%d_%d" % (a, m), w_bf[(a, m)][:], P)
             w_q[(a, m)] = (words[:], scales[:])
 
-        for a, m in ((0, 0), (0, 1), (1, 0), (2, 0), (3, 0), (1, 1)):
-            round_w(nc.scalar.copy, a, m)
-        round_x(0)
+        for a in range(PASSES):
+            round_w(nc.scalar.copy, a, 0)
+        round_w(nc.scalar.copy, 0, 1)
+        round_x(0, held([P, HALF, PACK], BF16, "x_bf_last0"))
         quantize_w(0, 0)
-        round_x(1)
-        quantize_w(0, 1)
+        round_x(1, placed([P, HALF, PACK], BF16, "x_bf_last1", 0))
         quantize_x(0)
         quantize_w(1, 0)
         quantize_x(1)
-        round_w(nc.vector.tensor_copy, 2, 1)
         quantize_w(2, 0)
         quantize_w(3, 0)
-        quantize_w(2, 1)
-        round_w(nc.vector.tensor_copy, 3, 1)
+        round_w(nc.vector.tensor_copy, 1, 1)
+        quantize_w(0, 1)
+        round_w(nc.vector.tensor_copy, 2, 1)
         quantize_w(1, 1)
+        round_w(nc.vector.tensor_copy, 3, 1)
+        quantize_w(2, 1)
         quantize_w(3, 1)
 
-        acc = {(m, h): bank([P, HALF], "acc%d_%d" % (m, h), ACC_BANK[2 * m + h]) for m in range(M_TILES) for h in range(2)}
-        for a, m in ((0, 0), (0, 1), (1, 0), (2, 0), (3, 0), (2, 1), (1, 1), (3, 1)):
-            for h in range(2):
-                nc.tensor.matmul_mx(
-                    out=acc[(m, h)][:],
-                    lhsT=w_q[(a, m)][0].bitcast(FP8X4),
-                    lhsT_scale=w_q[(a, m)][1],
-                    rhs=x_q[(a, h)][0].bitcast(FP8X4),
-                    rhs_scale=x_q[(a, h)][1],
-                    start=(a == 0),
-                    stop=(a == LAST),
-                )
-
-        y = [held([P, S], F32, "y%d" % m) for m in range(M_TILES)]
-        fetched = [held([P, V], F32, "fetched%d" % d) for d in range(D)]
-        nc.scalar.activation(out=y[0][:, 0:HALF], in_=acc[(0, 0)][:], func=RELU, bias=bias[0])
-        nc.vector.tensor_scalar(y[0][:, HALF:S], acc[(0, 1)][:], bias[0], 0.0, ADD, MAX)
-        for d, engine in enumerate(("vector", "scalar", "vector")):
-            gather(engine, fetched[d][:], y[0][:], places[d][:])
-        for h in range(2):
-            nc.scalar.activation(out=y[1][:, h * HALF : (h + 1) * HALF], in_=acc[(1, h)][:], func=RELU, bias=bias[1])
+        acc = {(m, h): bank([P, HALF], "acc%d_%d" % (m, h), 2 * m + h) for m in range(M_TILES) for h in range(2)}
+        for m in range(M_TILES):
+            for a in range(PASSES):
+                for h in range(2):
+                    nc.tensor.matmul_mx(
+                        out=acc[(m, h)][:],
+                        lhsT=w_q[(a, m)][0].bitcast(FP8X4),
+                        lhsT_scale=w_q[(a, m)][1],
+                        rhs=x_q[(a, h)][0].bitcast(FP8X4),
+                        rhs_scale=x_q[(a, h)][1],
+                        start=(a == 0),
+                        stop=(a == LAST),
+                    )
 
         spans = [slice(h * P, (h + 1) * P) for h in range(V_TILES)]
-        scaled = held([P, D, V], F32, "scaled")
-        sums = [bank([P, P], "sum%d" % h, ACC_BANK[h]) for h in range(V_TILES)]
-        for d in range(D):
-            turned = bank([P, V], "turned%d" % d, TURN_BANK + d)
+        for m in range(M_TILES):
+            y = held([P, S], F32, "y%d" % m)
+            for h in range(2):
+                nc.scalar.activation(out=y[:, h * HALF : (h + 1) * HALF], in_=acc[(m, h)][:], func=RELU, bias=bias[m])
+            fetched = [held([P, V], F32, "fetched%d_%d" % (m, d)) for d in range(2)]
+            products = [held([P, V], F32, "product%d_%d" % (m, d)) for d in range(D)]
+            if m == 0:
+                last_w = (M_TILES * PASSES - 1) * W_RAW_BYTES
+                products[0] = placed([P, V], F32, "product0_0_late", last_w)
+                products[2] = placed([P, V], F32, "product0_2_late", last_w + V * 4)
+            for d in range(2):
+                gather("scalar", fetched[d][:], y[:], places[d][:])
+            nc.vector.tensor_tensor(products[2][:], y[:].indirect(places[2][:]), gates[:, 2, :], MULT)
+            for d in range(2):
+                nc.vector.tensor_tensor(products[d][:], fetched[d][:], gates[:, d, :], MULT)
+            partial = held([P, V], F32, "partial%d" % m)
+            total = held([P, V], F32, "total%d" % m)
             for span in spans:
-                nc.tensor.transpose(turned[:, span], fetched[d][:, span], identity[:])
-            for h, span in enumerate(spans):
-                nc.scalar.activation(out=scaled[:, d, span], in_=turned[:, span], func=COPY, scale=columns[h][:, d : d + 1])
-        fetched_last = placed([P, V], F32, "fetched_last", AFTER_SCALING)
-        for span in spans:
-            gather("scalar", fetched_last[:, span], y[1][:], entries(places[D - 1], span.start, span.stop))
-        for d in range(D):
-            for h, span in enumerate(spans):
-                nc.tensor.matmul(sums[h][:], scaled[:, d, span], identity[:], start=(d == 0), stop=(d == D - 1), is_transpose=True)
-        total0 = held([P, V], F32, "total0")
-        for h, span in enumerate(spans):
-            nc.scalar.copy(out=total0[:, span], in_=sums[h][:])
-        nc.sync.dma_start(out=out[0:P, :], in_=total0[:])
-
-        products = [held([P, V], F32, "product%d" % d) for d in range(D)]
-        for d in range(D - 1):
-            nc.vector.tensor_tensor(products[d][:], y[1][:].indirect(places[d][:]), gates[:, d, :], MULT)
-        partial = held([P, V], F32, "partial")
-        total1 = held([P, V], F32, "total1")
-        nc.vector.tensor_tensor(products[D - 1][:, spans[0]], fetched_last[:, spans[0]], gates[:, D - 1, spans[0]], MULT)
-        nc.vector.tensor_tensor(partial[:], products[0][:], products[1][:], ADD)
-        nc.vector.tensor_tensor(products[D - 1][:, spans[1]], fetched_last[:, spans[1]], gates[:, D - 1, spans[1]], MULT)
-        for span in spans:
-            nc.vector.tensor_tensor(total1[:, span], partial[:, span], products[D - 1][:, span], ADD)
-        nc.sync.dma_start(out=out[P:N, :], in_=total1[:])
+                nc.vector.tensor_tensor(partial[:, span], products[2][:, span], products[0][:, span], ADD)
+            for span in spans:
+                nc.vector.tensor_tensor(total[:, span], partial[:, span], products[1][:, span], ADD)
+            nc.sync.dma_start(out=out[m * P : (m + 1) * P, :], in_=total[:])

@@ -29,15 +29,11 @@ LIST_ROWS = 16
 BANK = 2048
 RUN = 2
 
-X_LOADS = ((2, 2), (2, 2), (2, 2), (2, 1, 1))
-GATHERED_BY = (
-    ("vector", "scalar", "vector", "scalar"),
-    ("scalar", "scalar", "vector", "scalar"),
-    ("scalar", "scalar", "vector", "scalar"),
-    ("scalar", "both", "both", "both"),
-)
+X_LOADS = ((2, 2), (2, 2), (2, 1, 1), (1, 1, 1, 1))
+VECTOR_SHARE = ((512, 0, 256, 256), (0, 128, 256, 256), (0, 0, 512, 256), (0, 0, 384, 256))
 
 W_RAW_BYTES = PACK * P * 4
+W_BF_AT = {}
 
 
 def interleave(copy, grouped, raw):
@@ -74,7 +70,7 @@ def tile_picked_sub_lin_relu_sub_e_kernel(tc, xT, w, b, gate, offs, pos1, pos2, 
         rows = held([P, V], F32, "rows")
         identity = held([P, P], F32, "identity")
         columns = held([P, V_TILES, D + 1], F32, "columns")
-        gates = held([P, D, V], F32, "gates")
+        last_gate = held([P, V], F32, "last_gate")
         w_raw = {
             (a, m): placed([P, PACK, P], F32, "w_raw%d_%d" % (a, m), (m * PASSES + a) * W_RAW_BYTES)
             for m in range(M_TILES)
@@ -115,11 +111,11 @@ def tile_picked_sub_lin_relu_sub_e_kernel(tc, xT, w, b, gate, offs, pos1, pos2, 
             nc.tensor.transpose(turned_rows[:, h, :], rows[:, h * P : (h + 1) * P], identity[:])
         nc.scalar.copy(out=columns[:], in_=turned_rows[:, :, 0 : D + 1])
         bias = [columns[:, m, D : D + 1] for m in range(M_TILES)]
-        for d in range(D):
-            spread = bank([P, V], "spread%d" % d, 5 + d)
+        gates = [bank([P, V], "gates%d" % d, 5 + d) for d in range(D)]
+        for d in reversed(range(D)):
             for h in range(V_TILES):
-                nc.tensor.transpose(spread[:, h * P : (h + 1) * P], columns[:, h, d : d + 1].to_broadcast([P, P]), identity[:])
-            nc.vector.tensor_copy(out=gates[:, d, :], in_=spread[:])
+                nc.tensor.transpose(gates[d][:, h * P : (h + 1) * P], columns[:, h, d : d + 1].to_broadcast([P, P]), identity[:])
+        nc.vector.tensor_copy(out=last_gate[:], in_=gates[D - 1][:])
 
         def gather(engine, dst, window, picks):
             if engine == "vector":
@@ -138,22 +134,23 @@ def tile_picked_sub_lin_relu_sub_e_kernel(tc, xT, w, b, gate, offs, pos1, pos2, 
 
         def pick(a):
             picked = held([P, PACK, S], F32, "picked%d" % a)
-            for j, engine in enumerate(GATHERED_BY[a]):
-                if engine == "both":
-                    gather("scalar", picked[:, j, 0:HALF], plane[(a, j)], entries(offsets, 0, HALF))
-                    gather("vector", picked[:, j, HALF:S], plane[(a, j)], entries(offsets, HALF, S))
-                else:
-                    gather(engine, picked[:, j, :], plane[(a, j)], offsets[:])
+            for j, share in enumerate(VECTOR_SHARE[a]):
+                cut = S - share
+                if cut > 0:
+                    gather("scalar", picked[:, j, 0:cut], plane[(a, j)], entries(offsets, 0, cut))
+                if share > 0:
+                    gather("vector", picked[:, j, cut:S], plane[(a, j)], entries(offsets, cut, S))
             return picked
 
         x_q = {}
         for a in range(LAST):
             picked = pick(a)
-            grouped = held([P, S, PACK], BF16, "x_bf%d" % a)
-            interleave(nc.vector.tensor_copy, grouped[:], picked[:])
-            words, scales = quantize("x%d" % a, grouped[:], S)
+            grouped = [held([P, HALF, PACK], BF16, "x_bf%d_%d" % (a, h)) for h in range(2)]
             for h in range(2):
-                x_q[(a, h)] = (words[:, h * HALF : (h + 1) * HALF], scales[:, h * HALF : (h + 1) * HALF])
+                interleave(nc.vector.tensor_copy, grouped[h][:], picked[:, :, h * HALF : (h + 1) * HALF])
+            for h in range(2):
+                words, scales = quantize("x%d_%d" % (a, h), grouped[h][:], HALF)
+                x_q[(a, h)] = (words[:], scales[:])
 
         picked_last = pick(LAST)
         x_bf = {}
@@ -163,14 +160,17 @@ def tile_picked_sub_lin_relu_sub_e_kernel(tc, xT, w, b, gate, offs, pos1, pos2, 
             interleave(nc.vector.tensor_copy, grouped[:], picked_last[:, :, h * HALF : (h + 1) * HALF])
 
         def quantize_x(h):
-            words, scales = quantize("x_last%d" % h, x_bf[h][:], HALF, W_RAW_BYTES if h == 0 else None)
+            words, scales = quantize("x_last%d" % h, x_bf[h][:], HALF, (h + 1) * W_RAW_BYTES)
             x_q[(LAST, h)] = (words[:], scales[:])
 
         w_bf = {}
         w_q = {}
 
         def round_w(copy, a, m):
-            w_bf[(a, m)] = held([P, P, PACK], BF16, "w_bf%d_%d" % (a, m))
+            if (a, m) in W_BF_AT:
+                w_bf[(a, m)] = placed([P, P, PACK], BF16, "w_bf%d_%d" % (a, m), W_BF_AT[(a, m)])
+            else:
+                w_bf[(a, m)] = held([P, P, PACK], BF16, "w_bf%d_%d" % (a, m))
             interleave(copy, w_bf[(a, m)][:], w_raw[(a, m)][:])
 
         def quantize_w(a, m):
@@ -183,10 +183,10 @@ def tile_picked_sub_lin_relu_sub_e_kernel(tc, xT, w, b, gate, offs, pos1, pos2, 
         round_x(0, held([P, HALF, PACK], BF16, "x_bf_last0"))
         quantize_w(0, 0)
         round_x(1, placed([P, HALF, PACK], BF16, "x_bf_last1", 0))
-        quantize_x(0)
         quantize_w(1, 0)
-        quantize_x(1)
+        quantize_x(0)
         quantize_w(2, 0)
+        quantize_x(1)
         quantize_w(3, 0)
         round_w(nc.vector.tensor_copy, 1, 1)
         quantize_w(0, 1)
@@ -223,9 +223,9 @@ def tile_picked_sub_lin_relu_sub_e_kernel(tc, xT, w, b, gate, offs, pos1, pos2, 
                 products[2] = placed([P, V], F32, "product0_2_late", last_w + V * 4)
             for d in range(2):
                 gather("scalar", fetched[d][:], y[:], places[d][:])
-            nc.vector.tensor_tensor(products[2][:], y[:].indirect(places[2][:]), gates[:, 2, :], MULT)
+            nc.vector.tensor_tensor(products[2][:], y[:].indirect(places[2][:]), last_gate[:], MULT)
             for d in range(2):
-                nc.vector.tensor_tensor(products[d][:], fetched[d][:], gates[:, d, :], MULT)
+                nc.vector.tensor_tensor(products[d][:], fetched[d][:], gates[d][:], MULT)
             partial = held([P, V], F32, "partial%d" % m)
             total = held([P, V], F32, "total%d" % m)
             for span in spans:

@@ -29,8 +29,8 @@ LIST_ROWS = 16
 BANK = 2048
 RUN = 2
 
-X_LOADS = ((2, 2), (2, 2), (2, 1, 1), (1, 1, 1, 1))
-VECTOR_SHARE = ((512, 0, 256, 256), (0, 128, 256, 256), (0, 0, 512, 256), (0, 0, 384, 256))
+X_LOADS = ((2, 2), (2, 2), (2, 2), (2, 2))
+VECTOR_SHARE = ((512, 0, 256, 256), (0, 256, 256, 256), (0, 256, 256, 256), (0, 256, 256, 256))
 
 W_RAW_BYTES = PACK * P * 4
 W_BF_AT = {}

from contextlib import ExitStack

import concourse.mybir as mybir
from concourse.masks import make_identity

K, T, D, S, V, N = 2048, 1024, 3, 512, 256, 256
FLOPS = 2 * K * N * S

F32 = mybir.dt.float32
BF16 = mybir.dt.bfloat16
U32 = mybir.dt.uint32
U16 = mybir.dt.uint16
U8 = mybir.dt.uint8
FP8X4 = mybir.dt.float8_e4m3fn_x4
RELU = mybir.ActivationFunctionType.Relu
COPY = mybir.ActivationFunctionType.Copy
MULT = mybir.AluOpType.mult
ADD = mybir.AluOpType.add

P = 128
PACK = 4
K_PASS = P * PACK
PASSES = K // K_PASS
LAST = PASSES - 1
M_TILES = N // P
V_TILES = V // P
HALF = S // 2
LIST_ROWS = 16
BANK = 2048
RUN = 2

X_LOADS = ((2, 2), (2, 2), (2, 2), (2, 2))
VECTOR_SHARE = ((512, 0, 256, 256), (0, 256, 256, 256), (0, 256, 256, 256), (0, 256, 256, 256))

W_RAW_BYTES = PACK * P * 4
W_BF_AT = {}


def interleave(copy, grouped, raw):
    copy(
        out=grouped.rearrange("p (c i) j -> p c j i", i=RUN),
        in_=raw.rearrange("p j (c i) -> p c j i", i=RUN),
    )


def tile_picked_sub_lin_relu_sub_e_kernel(tc, xT, w, b, gate, offs, pos1, pos2, pos3, out):
    nc = tc.nc
    with ExitStack() as ctx:
        keep = ctx.enter_context(tc.tile_pool(name="keep", bufs=1))
        order = ctx.enter_context(tc.tile_pool(name="order", bufs=1))
        psum = ctx.enter_context(tc.psum_pool(name="psum", bufs=1))

        def held(shape, dtype, name):
            return keep.tile(shape, dtype, name=name, align_bytes=64)

        def placed(shape, dtype, name, offset):
            return order.tile(shape, dtype, name=name, align_bytes=64, offset=offset)

        def bank(shape, name, number):
            return psum.tile(shape, F32, name=name, offset=number * BANK)

        def k_rows(src, a):
            return src[a * K_PASS : (a + 1) * K_PASS, :].rearrange("(p j) c -> p j c", j=PACK)

        def entries(table, first, stop):
            return table[:, first // LIST_ROWS : stop // LIST_ROWS]

        offsets = held([P, S // LIST_ROWS], U16, "offsets")
        places = [held([P, V // LIST_ROWS], U16, "places%d" % d) for d in range(D)]
        rows = held([P, V], F32, "rows")
        identity = held([P, P], F32, "identity")
        columns = held([P, V_TILES, D + 1], F32, "columns")
        last_gate = held([P, V], F32, "last_gate")
        w_raw = {
            (a, m): placed([P, PACK, P], F32, "w_raw%d_%d" % (a, m), (m * PASSES + a) * W_RAW_BYTES)
            for m in range(M_TILES)
            for a in range(PASSES)
        }

        nc.gpsimd.memset(rows[:], 0.0)
        make_identity(nc, identity[:])

        plane = {}
        for a in range(PASSES):
            first = 0
            for count in X_LOADS[a]:
                raw = held([P, count, T], F32, "x_raw%d_%d" % (a, first))
                nc.sync.dma_start(out=raw[:], in_=k_rows(xT, a)[:, first : first + count, :])
                if (a, first) == (0, 0):
                    nc.sync.dma_start(offsets[:], offs)
                    nc.sync.dma_start(out=rows[0:D, :], in_=gate[:, 0, :])
                    nc.sync.dma_start(out=rows[D : D + 1, :], in_=b.rearrange("n o -> o n"))
                for j in range(count):
                    plane[(a, first + j)] = raw[:, j, :]
                first += count

        def load_w(a, m):
            nc.sync.dma_start(out=w_raw[(a, m)][:], in_=k_rows(w, a)[:, :, m * P : (m + 1) * P])

        for a in range(PASSES):
            load_w(a, 0)
        for a in range(LAST):
            load_w(a, 1)
        nc.sync.dma_start(places[0][:], pos1)
        load_w(LAST, 1)
        nc.sync.dma_start(places[2][:], pos3)
        nc.sync.dma_start(places[1][:], pos2)

        turned_rows = bank([P, V_TILES, P], "turned_rows", 4)
        for h in range(V_TILES):
            nc.tensor.transpose(turned_rows[:, h, :], rows[:, h * P : (h + 1) * P], identity[:])
        nc.scalar.copy(out=columns[:], in_=turned_rows[:, :, 0 : D + 1])
        bias = [columns[:, m, D : D + 1] for m in range(M_TILES)]
        gates = [bank([P, V], "gates%d" % d, 5 + d) for d in range(D)]
        for d in reversed(range(D)):
            for h in range(V_TILES):
                nc.tensor.transpose(gates[d][:, h * P : (h + 1) * P], columns[:, h, d : d + 1].to_broadcast([P, P]), identity[:])
        nc.vector.tensor_copy(out=last_gate[:], in_=gates[D - 1][:])

        def gather(engine, dst, window, picks):
            if engine == "vector":
                nc.vector.tensor_copy(dst, window.indirect(picks))
            else:
                nc.scalar.activation(dst, window.indirect(picks), COPY)

        def quantize(name, grouped, width, offset=None):
            if offset is None:
                words = held([P, width], U32, name + "_words")
            else:
                words = placed([P, width], U32, name + "_words", offset)
            scales = held([P, width], U8, name + "_scales")
            nc.vector.quantize_mx(out=words[:].bitcast(FP8X4), scales=scales[:], in_=grouped.rearrange("p c j -> p (c j)"))
            return words, scales

        def pick(a):
            picked = held([P, PACK, S], F32, "picked%d" % a)
            for j, share in enumerate(VECTOR_SHARE[a]):
                cut = S - share
                if cut > 0:
                    gather("scalar", picked[:, j, 0:cut], plane[(a, j)], entries(offsets, 0, cut))
                if share > 0:
                    gather("vector", picked[:, j, cut:S], plane[(a, j)], entries(offsets, cut, S))
            return picked

        x_q = {}
        for a in range(LAST):
            picked = pick(a)
            grouped = [held([P, HALF, PACK], BF16, "x_bf%d_%d" % (a, h)) for h in range(2)]
            for h in range(2):
                interleave(nc.vector.tensor_copy, grouped[h][:], picked[:, :, h * HALF : (h + 1) * HALF])
            for h in range(2):
                words, scales = quantize("x%d_%d" % (a, h), grouped[h][:], HALF)
                x_q[(a, h)] = (words[:], scales[:])

        picked_last = pick(LAST)
        x_bf = {}

        def round_x(h, grouped):
            x_bf[h] = grouped
            interleave(nc.vector.tensor_copy, grouped[:], picked_last[:, :, h * HALF : (h + 1) * HALF])

        def quantize_x(h):
            words, scales = quantize("x_last%d" % h, x_bf[h][:], HALF, (h + 1) * W_RAW_BYTES)
            x_q[(LAST, h)] = (words[:], scales[:])

        w_bf = {}
        w_q = {}

        def round_w(copy, a, m):
            if (a, m) in W_BF_AT:
                w_bf[(a, m)] = placed([P, P, PACK], BF16, "w_bf%d_%d" % (a, m), W_BF_AT[(a, m)])
            else:
                w_bf[(a, m)] = held([P, P, PACK], BF16, "w_bf%d_%d" % (a, m))
            interleave(copy, w_bf[(a, m)][:], w_raw[(a, m)][:])

        def quantize_w(a, m):
            words, scales = quantize("w%d_%d" % (a, m), w_bf[(a, m)][:], P)
            w_q[(a, m)] = (words[:], scales[:])

        for a in range(PASSES):
            round_w(nc.scalar.copy, a, 0)
        round_w(nc.scalar.copy, 0, 1)
        round_x(0, held([P, HALF, PACK], BF16, "x_bf_last0"))
        quantize_w(0, 0)
        round_x(1, placed([P, HALF, PACK], BF16, "x_bf_last1", 0))
        quantize_w(1, 0)
        quantize_x(0)
        quantize_w(2, 0)
        quantize_x(1)
        quantize_w(3, 0)
        round_w(nc.vector.tensor_copy, 1, 1)
        quantize_w(0, 1)
        round_w(nc.vector.tensor_copy, 2, 1)
        quantize_w(1, 1)
        round_w(nc.vector.tensor_copy, 3, 1)
        quantize_w(2, 1)
        quantize_w(3, 1)

        acc = {(m, h): bank([P, HALF], "acc%d_%d" % (m, h), 2 * m + h) for m in range(M_TILES) for h in range(2)}
        for m in range(M_TILES):
            for a in range(PASSES):
                for h in range(2):
                    nc.tensor.matmul_mx(
                        out=acc[(m, h)][:],
                        lhsT=w_q[(a, m)][0].bitcast(FP8X4),
                        lhsT_scale=w_q[(a, m)][1],
                        rhs=x_q[(a, h)][0].bitcast(FP8X4),
                        rhs_scale=x_q[(a, h)][1],
                        start=(a == 0),
                        stop=(a == LAST),
                    )

        spans = [slice(h * P, (h + 1) * P) for h in range(V_TILES)]
        for m in range(M_TILES):
            y = held([P, S], F32, "y%d" % m)
            for h in range(2):
                nc.scalar.activation(out=y[:, h * HALF : (h + 1) * HALF], in_=acc[(m, h)][:], func=RELU, bias=bias[m])
            fetched = [held([P, V], F32, "fetched%d_%d" % (m, d)) for d in range(2)]
            products = [held([P, V], F32, "product%d_%d" % (m, d)) for d in range(D)]
            if m == 0:
                last_w = (M_TILES * PASSES - 1) * W_RAW_BYTES
                products[0] = placed([P, V], F32, "product0_0_late", last_w)
                products[2] = placed([P, V], F32, "product0_2_late", last_w + V * 4)
            for d in range(2):
                gather("scalar", fetched[d][:], y[:], places[d][:])
            nc.vector.tensor_tensor(products[2][:], y[:].indirect(places[2][:]), last_gate[:], MULT)
            for d in range(2):
                nc.vector.tensor_tensor(products[d][:], fetched[d][:], gates[d][:], MULT)
            partial = held([P, V], F32, "partial%d" % m)
            total = held([P, V], F32, "total%d" % m)
            for span in spans:
                nc.vector.tensor_tensor(partial[:, span], products[2][:, span], products[0][:, span], ADD)
            for span in spans:
                nc.vector.tensor_tensor(total[:, span], partial[:, span], products[1][:, span], ADD)
            nc.sync.dma_start(out=out[m * P : (m + 1) * P, :], in_=total[:])
